import numpy as np
import ml_dtypes


def mxq(x, axis, fmt="e4m3"):
    dtype, down = {"e4m3": (ml_dtypes.float8_e4m3fn, 7), "e5m2": (ml_dtypes.float8_e5m2, 14)}[fmt]
    v = np.moveaxis(np.asarray(x, np.float32).astype(ml_dtypes.bfloat16).astype(np.float64), axis, -1)
    blocks = v.reshape(v.shape[:-1] + (-1, 32))
    amax = np.abs(blocks).max(-1, keepdims=True)
    byte = np.maximum(np.where(amax > 0, np.frexp(amax)[1] - 1 + 127, 0) - down, 1)
    scale = np.exp2(byte - 127.0)
    codes = (blocks / scale).astype(np.float32).astype(dtype).astype(np.float64)
    return np.moveaxis((codes * scale).reshape(v.shape), -1, axis)


WIDE = False


def mx_kscale(k):
    if not WIDE:
        return np.ones(k)
    levels = np.array([10, -10, 5, -5, 0])
    if k % 512:
        return np.exp2(np.random.permutation(np.resize(levels, k // 32))).repeat(32)
    a = np.empty((k // 512, 16))
    for p in range(k // 512):
        a[p, :8] = np.random.permutation(np.resize(levels, 8))
        for g in range(8):
            far = levels[np.abs(levels - a[p, g]) >= 10]
            a[p, g + 8] = far[np.random.randint(len(far))]
    return np.exp2(a.ravel()).repeat(32)


def f64(x):
    return np.asarray(x).astype(np.float64)


def striped(idx):
    return np.tile(idx.reshape(-1, 16).T, (8, 1)).astype(np.uint16)


def unstriped(offs):
    return offs[:16].T.reshape(-1).astype(np.int64)


def pack_weight(w):
    k, n = w.shape
    w = f64(np.asarray(w, np.float32).astype(ml_dtypes.bfloat16)).reshape(k // 32, 32, n)
    amax = np.abs(w).max(1)
    byte = np.clip(np.where(amax > 0, np.frexp(amax)[1] - 1 + 127 - 7, 1), 1, 254)
    scaled = (w * np.exp2(127.0 - byte)[:, None, :]).reshape(k, n).astype(np.float32)
    words = np.ascontiguousarray(scaled.reshape(k // 512, 128, 4, n).transpose(0, 1, 3, 2)).astype(ml_dtypes.float8_e4m3fn).view(np.uint8)
    return words, np.ascontiguousarray(byte.astype(np.uint8).reshape(k // 512, 16, n))


def unpack_weight(words, scales):
    g, p, n, _ = words.shape
    vals = np.ascontiguousarray(words).view(ml_dtypes.float8_e4m3fn).astype(np.float64) * np.repeat(np.exp2(scales.astype(np.float64) - 127.0), 8, axis=1)[..., None]
    return vals.transpose(0, 1, 3, 2).reshape(g * 512, n)


def relu(v):
    return np.maximum(v, 0.0)


K, T, S, D, V, H, G, R = 1024, 2048, 512, 2, 256, 512, 2048, 512
P = 2 ** 7


def setup_inputs():
    n = np.random.standard_normal
    s = mx_kscale(K)[:, None]
    u = mx_kscale(H)
    near = np.random.permutation(S)
    packed_xT = pack_weight(n((K, T)) * s)
    packed_vT = pack_weight(n((H, G)) / np.sqrt(H) / u[:, None])
    return {
        "x_words": packed_xT[0],
        "x_scales": packed_xT[1],
        "w1": (n((K, H)) / np.sqrt(K) / s * u).astype(np.float32),
        "gate": (np.tile(np.random.uniform(0.2, 1.0, (D, 1, V)) / np.sqrt(D), (1, P, 1))).astype(np.float32),
        "v_words": packed_vT[0],
        "v_scales": packed_vT[1],
        "offs": striped(np.random.permutation(T)[:S]),
        "pos1": striped(near[:V]),
        "pos2": striped(near[V:]),
        "cand": striped(np.random.permutation(G)[:R]),
    }


def reference(x_words, x_scales, w1, gate, v_words, v_scales, offs, pos1, pos2, cand):
    xq = unpack_weight(x_words, x_scales)[:, unstriped(offs)]
    h = relu(mxq(f64(w1), 0, "e4m3").T @ xq)
    z = h[:, unstriped(pos1)] * f64(gate)[0, :1] + h[:, unstriped(pos2)] * f64(gate)[1, :1]
    v_cand = unpack_weight(v_words, v_scales)[:, unstriped(cand)]
    y = mxq(z, 0, "e4m3").T @ v_cand
    e = np.exp(y - y.max(axis=1, keepdims=True))
    return e / e.sum(axis=1, keepdims=True)

@@ -1,0 +1,144 @@
+from contextlib import ExitStack
+
+import concourse.mybir as mybir
+
+F32 = mybir.dt.float32
+BF16 = mybir.dt.bfloat16
+I32 = mybir.dt.int32
+U32 = mybir.dt.uint32
+U16 = mybir.dt.uint16
+U8 = mybir.dt.uint8
+FP8X4 = mybir.dt.float8_e4m3fn_x4
+ALU = mybir.AluOpType
+ACT = mybir.ActivationFunctionType
+AXIS = mybir.AxisListType
+
+K, T, S, V, H, G, R = 1024, 2048, 512, 256, 512, 2048, 512
+P = 128
+PACK = 4
+PASSES = K // (P * PACK)
+HALVES = V // P
+FLOPS = 2 * K * H * S + 2 * H * V * R
+
+
+def tile_picked_zcbow_relu_p_kernel(tc, x_words, x_scales, w1, gate, v_words, v_scales, offs, pos1, pos2, cand, out):
+    nc = tc.nc
+    with ExitStack() as ctx:
+        keep = ctx.enter_context(tc.tile_pool(name="keep", bufs=1))
+        psum = ctx.enter_context(tc.psum_pool(name="psum", bufs=1))
+
+        offs_sb = keep.tile([P, S // 16], U16, name="offs_sb")
+        pos_sb = [keep.tile([P, V // 16], U16, name="pos_sb%d" % d) for d in range(2)]
+        cand_sb = keep.tile([P, R // 16], U16, name="cand_sb")
+        w_raw = [keep.tile([P, PACK, H], F32, name="w_raw%d" % g) for g in range(PASSES)]
+        x_table = [keep.tile([P, T], I32, name="x_table%d" % g) for g in range(PASSES)]
+        v_table = keep.tile([P, G], I32, name="v_table")
+        xs_table = keep.tile([P, T], U8, name="xs_table")
+        vs_table = keep.tile([P, G], U8, name="vs_table")
+        gate_sb = keep.tile([P, 2, V], F32, name="gate_sb")
+
+        nc.vector.memset(xs_table[:].bitcast(I32), 0)
+        nc.vector.memset(vs_table[:].bitcast(I32), 0)
+        for q in range(4):
+            nc.gpsimd.dma_start(out=xs_table[32 * q : 32 * q + 8, :].bitcast(I32), in_=x_scales[:, 4 * q : 4 * q + 4, :].bitcast(I32))
+        for q in range(4):
+            nc.gpsimd.dma_start(out=vs_table[32 * q + 8 : 32 * q + 12, :].bitcast(I32), in_=v_scales[0, 4 * q : 4 * q + 4, :].bitcast(I32))
+
+        for g in range(PASSES):
+            nc.sync.dma_start(out=w_raw[g][:], in_=w1[g * 512 : (g + 1) * 512, :].rearrange("(p j) c -> p j c", j=PACK))
+        nc.sync.dma_start(offs_sb[:], offs)
+        nc.sync.dma_start(cand_sb[:], cand)
+        for g in range(PASSES):
+            nc.sync.dma_start(out=x_table[g][:], in_=x_words[g].rearrange("p n t -> p (n t)").bitcast(I32))
+        nc.sync.dma_start(pos_sb[0][:], pos1)
+        nc.sync.dma_start(pos_sb[1][:], pos2)
+        nc.sync.dma_start(out=gate_sb[:], in_=gate.rearrange("d p v -> p d v"))
+        nc.sync.dma_start(out=v_table[:], in_=v_words[0].rearrange("p n t -> p (n t)").bitcast(I32))
+
+        w_codes = []
+        w_scale = []
+        for g in range(PASSES):
+            grouped = keep.tile([P, H * PACK], BF16, name="w_grouped%d" % g, align_bytes=64)
+            nc.scalar.activation(
+                out=grouped[:].rearrange("p (t m j) -> p m j t", t=PACK, j=PACK),
+                in_=w_raw[g][:].rearrange("p j (m t) -> p m j t", t=PACK),
+                func=ACT.Copy,
+            )
+            codes = keep.tile([P, H], U32, name="w_codes%d" % g, align_bytes=64)
+            scale = keep.tile([P, H], U8, name="w_scale%d" % g, align_bytes=64)
+            nc.vector.quantize_mx(out=codes[:].bitcast(FP8X4), scales=scale[:], in_=grouped[:])
+            w_codes.append(codes)
+            w_scale.append(scale)
+
+        x_scale = keep.tile([P, S], U8, name="x_scale", align_bytes=64)
+        nc.vector.tensor_copy(x_scale[:], xs_table[:].indirect(offs_sb[:]))
+        v_scale = keep.tile([P, R], U8, name="v_scale", align_bytes=64)
+        nc.vector.tensor_copy(v_scale[:], vs_table[:].indirect(cand_sb[:]))
+        x_codes = []
+        for g in range(PASSES):
+            codes = keep.tile([P, S], U32, name="x_codes%d" % g, align_bytes=64)
+            nc.vector.tensor_copy(codes[:], x_table[g][:].bitcast(U32).indirect(offs_sb[:]))
+            x_codes.append(codes)
+
+        h_ps = [psum.tile([P, S], F32, name="h_ps%d" % j) for j in range(PACK)]
+        for g in range(PASSES):
+            for j in range(PACK):
+                cols = slice(j * P, (j + 1) * P)
+                nc.tensor.matmul_mx(
+                    out=h_ps[j][:],
+                    lhsT=w_codes[g][:, cols].bitcast(FP8X4),
+                    lhsT_scale=w_scale[g][:, cols],
+                    rhs=x_codes[g][:].bitcast(FP8X4),
+                    rhs_scale=x_scale[4 * g :, :],
+                    start=(g == 0),
+                    stop=(g == PASSES - 1),
+                )
+
+        terms = [keep.tile([P, PACK, V], F32, name="terms%d" % d) for d in range(2)]
+        for j in range(PACK):
+            h_sb = keep.tile([P, S], F32, name="h_sb%d" % j)
+            nc.scalar.activation(out=h_sb[:], in_=h_ps[j][:], func=ACT.Relu)
+            for d in range(2):
+                nc.vector.tensor_tensor(terms[d][:, j, :], h_sb[:].indirect(pos_sb[d][:]), gate_sb[:, d, :], ALU.mult)
+
+        v_codes = keep.tile([P, R], U32, name="v_codes", align_bytes=64)
+        nc.vector.tensor_copy(v_codes[:], v_table[:].bitcast(U32).indirect(cand_sb[:]))
+
+        z_grouped = []
+        for half in range(HALVES):
+            cols = slice(half * P, (half + 1) * P)
+            grouped = keep.tile([P, P * PACK], BF16, name="z_grouped%d" % half, align_bytes=64)
+            nc.vector.tensor_tensor(
+                grouped[:].rearrange("p (c i j) -> p c j i", i=4, j=PACK),
+                terms[0][:, :, cols].rearrange("p j (c i) -> p c j i", i=4),
+                terms[1][:, :, cols].rearrange("p j (c i) -> p c j i", i=4),
+                ALU.add,
+            )
+            z_grouped.append(grouped)
+        y_ps = []
+        for half in range(HALVES):
+            codes = keep.tile([P, P], U32, name="z_codes%d" % half, align_bytes=64)
+            scale = keep.tile([P, P], U8, name="z_scale%d" % half, align_bytes=64)
+            nc.vector.quantize_mx(out=codes[:].bitcast(FP8X4), scales=scale[:], in_=z_grouped[half][:])
+            y = psum.tile([P, R], F32, name="y_ps%d" % half)
+            nc.tensor.matmul_mx(
+                out=y[:],
+                lhsT=codes[:].bitcast(FP8X4),
+                lhsT_scale=scale[:],
+                rhs=v_codes[:].bitcast(FP8X4),
+                rhs_scale=v_scale[8:, :],
+                start=True,
+                stop=True,
+            )
+            y_ps.append(y)
+        for half in range(HALVES):
+            neg_max = keep.tile([P, 1], F32, name="neg_max%d" % half)
+            nc.vector.tensor_reduce(out=neg_max[:], in_=y_ps[half][:], axis=AXIS.X, op=ALU.max, negate=True)
+            e = keep.tile([P, R], F32, name="e%d" % half)
+            total = keep.tile([P, 1], F32, name="total%d" % half)
+            nc.scalar.activation(out=e[:], in_=y_ps[half][:], func=ACT.Exp, bias=neg_max[:], accum_out=total[:])
+            inv = keep.tile([P, 1], F32, name="inv%d" % half)
+            nc.vector.reciprocal(out=inv[:], in_=total[:])
+            res = keep.tile([P, R], F32, name="res%d" % half)
+            nc.vector.tensor_scalar(out=res[:], in0=e[:], scalar1=inv[:], scalar2=None, op0=ALU.mult)
+            nc.sync.dma_start(out=out[half * P : (half + 1) * P, :], in_=res[:])

@@ -34,31 +34,37 @@ def tile_picked_zcbow_relu_p_kernel(tc, x_words, x_scales, w1, gate, v_words, v_
         x_table = [keep.tile([P, T], I32, name="x_table%d" % g) for g in range(PASSES)]
         v_table = keep.tile([P, G], I32, name="v_table")
         xs_table = keep.tile([P, T], U8, name="xs_table")
-        vs_table = keep.tile([P, G], U8, name="vs_table")
+        vs_table = keep.tile([P, G], U8, name="vs_table", tag="terms0")
         gate_sb = keep.tile([P, 2, V], F32, name="gate_sb")
 
         nc.vector.memset(xs_table[:].bitcast(I32), 0)
         nc.vector.memset(vs_table[:].bitcast(I32), 0)
-        for q in range(4):
-            nc.gpsimd.dma_start(out=xs_table[32 * q : 32 * q + 8, :].bitcast(I32), in_=x_scales[:, 4 * q : 4 * q + 4, :].bitcast(I32))
-        for q in range(4):
-            nc.gpsimd.dma_start(out=vs_table[32 * q + 8 : 32 * q + 12, :].bitcast(I32), in_=v_scales[0, 4 * q : 4 * q + 4, :].bitcast(I32))
 
-        for g in range(PASSES):
+        def load_w(g):
             nc.sync.dma_start(out=w_raw[g][:], in_=w1[g * 512 : (g + 1) * 512, :].rearrange("(p j) c -> p j c", j=PACK))
-        nc.sync.dma_start(offs_sb[:], offs)
-        nc.sync.dma_start(cand_sb[:], cand)
-        for g in range(PASSES):
+
+        def load_x(g):
             nc.sync.dma_start(out=x_table[g][:], in_=x_words[g].rearrange("p n t -> p (n t)").bitcast(I32))
+
+        load_w(0)
+        load_w(1)
+        nc.sync.dma_start(offs_sb[:], offs)
+        for q in range(4):
+            nc.sync.dma_start(out=xs_table[32 * q : 32 * q + 8, :].bitcast(I32), in_=x_scales[:, 4 * q : 4 * q + 4, :].bitcast(I32))
+        load_x(0)
+        nc.sync.dma_start(cand_sb[:], cand)
         nc.sync.dma_start(pos_sb[0][:], pos1)
         nc.sync.dma_start(pos_sb[1][:], pos2)
+        load_x(1)
+        for q in range(4):
+            nc.sync.dma_start(out=vs_table[32 * q + 8 : 32 * q + 12, :].bitcast(I32), in_=v_scales[0, 4 * q : 4 * q + 4, :].bitcast(I32))
         nc.sync.dma_start(out=gate_sb[:], in_=gate.rearrange("d p v -> p d v"))
         nc.sync.dma_start(out=v_table[:], in_=v_words[0].rearrange("p n t -> p (n t)").bitcast(I32))
 
         w_codes = []
         w_scale = []
         for g in range(PASSES):
-            grouped = keep.tile([P, H * PACK], BF16, name="w_grouped%d" % g, align_bytes=64)
+            grouped = keep.tile([P, H * PACK], BF16, name="w_grouped%d" % g, tag="w_grouped%d" % g, align_bytes=64)
             nc.scalar.activation(
                 out=grouped[:].rearrange("p (t m j) -> p m j t", t=PACK, j=PACK),
                 in_=w_raw[g][:].rearrange("p j (m t) -> p m j t", t=PACK),
@@ -72,13 +78,14 @@ def tile_picked_zcbow_relu_p_kernel(tc, x_words, x_scales, w1, gate, v_words, v_
 
         x_scale = keep.tile([P, S], U8, name="x_scale", align_bytes=64)
         nc.vector.tensor_copy(x_scale[:], xs_table[:].indirect(offs_sb[:]))
-        v_scale = keep.tile([P, R], U8, name="v_scale", align_bytes=64)
-        nc.vector.tensor_copy(v_scale[:], vs_table[:].indirect(cand_sb[:]))
         x_codes = []
         for g in range(PASSES):
             codes = keep.tile([P, S], U32, name="x_codes%d" % g, align_bytes=64)
             nc.vector.tensor_copy(codes[:], x_table[g][:].bitcast(U32).indirect(offs_sb[:]))
             x_codes.append(codes)
+
+        v_scale = keep.tile([P, R], U8, name="v_scale", align_bytes=64)
+        nc.vector.tensor_copy(v_scale[:], vs_table[:].indirect(cand_sb[:]))
 
         h_ps = [psum.tile([P, S], F32, name="h_ps%d" % j) for j in range(PACK)]
         for g in range(PASSES):
@@ -94,7 +101,7 @@ def tile_picked_zcbow_relu_p_kernel(tc, x_words, x_scales, w1, gate, v_words, v_
                     stop=(g == PASSES - 1),
                 )
 
-        terms = [keep.tile([P, PACK, V], F32, name="terms%d" % d) for d in range(2)]
+        terms = [keep.tile([P, PACK, V], F32, name="terms%d" % d, tag="terms%d" % d) for d in range(2)]
         for j in range(PACK):
             h_sb = keep.tile([P, S], F32, name="h_sb%d" % j)
             nc.scalar.activation(out=h_sb[:], in_=h_ps[j][:], func=ACT.Relu)

@@ -16,136 +16,170 @@ AXIS = mybir.AxisListType
 K, T, S, V, H, G, R = 1024, 2048, 512, 256, 512, 2048, 512
 P = 128
 PACK = 4
+LIST = 16
+QUADRANT = 32
+SPREAD = 8
 PASSES = K // (P * PACK)
-HALVES = V // P
+WINDOW_TILES = V // P
+PARTS = 2
+BANK_SETS = 2
+HEAD = T // 4
 FLOPS = 2 * K * H * S + 2 * H * V * R
 
 
-def tile_picked_zcbow_relu_p_kernel(tc, x_words, x_scales, w1, gate, v_words, v_scales, offs, pos1, pos2, cand, out):
+def tile_picked_zcbow_relu_p_kernel(
+    tc, x_words, x_scales, w1, gate, v_words, v_scales, offs, pos1, pos2, cand, out
+):
     nc = tc.nc
     with ExitStack() as ctx:
         keep = ctx.enter_context(tc.tile_pool(name="keep", bufs=1))
         psum = ctx.enter_context(tc.psum_pool(name="psum", bufs=1))
 
-        offs_sb = keep.tile([P, S // 16], U16, name="offs_sb")
-        pos_sb = [keep.tile([P, V // 16], U16, name="pos_sb%d" % d) for d in range(2)]
-        cand_sb = keep.tile([P, R // 16], U16, name="cand_sb")
+        offs_sb = keep.tile([P, S // LIST], U16, name="offs_sb")
+        pos_sb = [keep.tile([P, V // LIST], U16, name="pos_sb%d" % d) for d in range(2)]
+        cand_sb = keep.tile([P, R // LIST], U16, name="cand_sb")
         w_raw = [keep.tile([P, PACK, H], F32, name="w_raw%d" % g) for g in range(PASSES)]
         x_table = [keep.tile([P, T], I32, name="x_table%d" % g) for g in range(PASSES)]
         v_table = keep.tile([P, G], I32, name="v_table")
-        xs_table = keep.tile([P, T], U8, name="xs_table")
-        vs_table = keep.tile([P, G], U8, name="vs_table", tag="terms0")
+        xs_table = keep.tile([P, PASSES, T], U8, name="xs_table")
+        vs_table = keep.tile([P, G], U8, name="vs_table")
+        x_scale = keep.tile([P, PASSES, S], U8, name="x_scale", align_bytes=64)
+        v_scale = keep.tile([P, R], U8, name="v_scale", align_bytes=64)
         gate_sb = keep.tile([P, 2, V], F32, name="gate_sb")
 
-        nc.vector.memset(xs_table[:].bitcast(I32), 0)
+        nc.gpsimd.memset(xs_table[:, 1, :].bitcast(I32), 0)
+        nc.vector.memset(xs_table[:, 0, :].bitcast(I32), 0)
         nc.vector.memset(vs_table[:].bitcast(I32), 0)
+        nc.vector.memset(x_scale[:].bitcast(I32), 0)
+        nc.vector.memset(v_scale[:].bitcast(I32), 0)
 
         def load_w(g):
-            nc.sync.dma_start(out=w_raw[g][:], in_=w1[g * 512 : (g + 1) * 512, :].rearrange("(p j) c -> p j c", j=PACK))
+            rows = w1[g * P * PACK : (g + 1) * P * PACK, :]
+            nc.sync.dma_start(out=w_raw[g][:], in_=rows.rearrange("(p j) c -> p j c", j=PACK))
 
-        def load_x(g):
-            nc.sync.dma_start(out=x_table[g][:], in_=x_words[g].rearrange("p n t -> p (n t)").bitcast(I32))
+        def words(table):
+            return table.rearrange("p n j -> p (n j)").bitcast(I32)
 
-        load_w(0)
-        load_w(1)
+        def list_part(list_sb, part):
+            columns = list_sb.shape[1] // PARTS
+            return list_sb[:, part * columns : (part + 1) * columns]
+
+        nc.sync.dma_start(out=x_table[0][:, :HEAD], in_=words(x_words[0])[:, :HEAD])
         nc.sync.dma_start(offs_sb[:], offs)
-        for q in range(4):
-            nc.sync.dma_start(out=xs_table[32 * q : 32 * q + 8, :].bitcast(I32), in_=x_scales[:, 4 * q : 4 * q + 4, :].bitcast(I32))
-        load_x(0)
         nc.sync.dma_start(cand_sb[:], cand)
+        nc.sync.dma_start(out=xs_table[0:P:SPREAD].bitcast(I32), in_=x_scales.rearrange("g n c -> n g c").bitcast(I32))
+        load_w(0)
+        nc.sync.dma_start(out=vs_table[SPREAD // 2 : P : SPREAD].bitcast(I32), in_=v_scales[0].bitcast(I32))
+        load_w(1)
+        nc.sync.dma_start(out=x_table[0][:, HEAD:], in_=words(x_words[0])[:, HEAD:])
+
+        xs_picked = keep.tile([P, PASSES, S], U8, name="xs_picked")
+        for g in range(PASSES):
+            nc.vector.tensor_copy(xs_picked[:, g, :], xs_table[:, g, :].indirect(offs_sb[:]))
+        for r in range(4):
+            nc.sync.dma_start(
+                out=x_scale[r:P:QUADRANT].bitcast(I32), in_=xs_picked[SPREAD * r : P : QUADRANT].bitcast(I32)
+            )
+        nc.sync.dma_start(out=x_table[1][:], in_=words(x_words[1]))
         nc.sync.dma_start(pos_sb[0][:], pos1)
         nc.sync.dma_start(pos_sb[1][:], pos2)
-        load_x(1)
-        for q in range(4):
-            nc.sync.dma_start(out=vs_table[32 * q + 8 : 32 * q + 12, :].bitcast(I32), in_=v_scales[0, 4 * q : 4 * q + 4, :].bitcast(I32))
         nc.sync.dma_start(out=gate_sb[:], in_=gate.rearrange("d p v -> p d v"))
-        nc.sync.dma_start(out=v_table[:], in_=v_words[0].rearrange("p n t -> p (n t)").bitcast(I32))
+        nc.sync.dma_start(out=v_table[:], in_=words(v_words[0]))
+        vs_picked = keep.tile([P, R], U8, name="vs_picked")
+        nc.vector.tensor_copy(vs_picked[:], vs_table[:].indirect(cand_sb[:]))
+        for r in range(4):
+            nc.sync.dma_start(
+                out=v_scale[r:P:QUADRANT].bitcast(I32),
+                in_=vs_picked[SPREAD * r + SPREAD // 2 : P : QUADRANT].bitcast(I32),
+            )
 
         w_codes = []
         w_scale = []
         for g in range(PASSES):
-            grouped = keep.tile([P, H * PACK], BF16, name="w_grouped%d" % g, tag="w_grouped%d" % g, align_bytes=64)
+            w_grouped = keep.tile([P, H * PACK], BF16, name="w_grouped%d" % g, align_bytes=64)
             nc.scalar.activation(
-                out=grouped[:].rearrange("p (t m j) -> p m j t", t=PACK, j=PACK),
-                in_=w_raw[g][:].rearrange("p j (m t) -> p m j t", t=PACK),
+                out=w_grouped[:].rearrange("p (lane m j) -> p m j lane", lane=PACK, j=PACK),
+                in_=w_raw[g][:].rearrange("p j (m lane) -> p m j lane", lane=PACK),
                 func=ACT.Copy,
             )
-            codes = keep.tile([P, H], U32, name="w_codes%d" % g, align_bytes=64)
-            scale = keep.tile([P, H], U8, name="w_scale%d" % g, align_bytes=64)
-            nc.vector.quantize_mx(out=codes[:].bitcast(FP8X4), scales=scale[:], in_=grouped[:])
-            w_codes.append(codes)
-            w_scale.append(scale)
+            w_codes.append(keep.tile([P, H], U32, name="w_codes%d" % g, align_bytes=64))
+            w_scale.append(keep.tile([P, H], U8, name="w_scale%d" % g, align_bytes=64))
+            nc.vector.quantize_mx(out=w_codes[g][:].bitcast(FP8X4), scales=w_scale[g][:], in_=w_grouped[:])
 
-        x_scale = keep.tile([P, S], U8, name="x_scale", align_bytes=64)
-        nc.vector.tensor_copy(x_scale[:], xs_table[:].indirect(offs_sb[:]))
-        x_codes = []
+        x_codes = {}
         for g in range(PASSES):
-            codes = keep.tile([P, S], U32, name="x_codes%d" % g, align_bytes=64)
-            nc.vector.tensor_copy(codes[:], x_table[g][:].bitcast(U32).indirect(offs_sb[:]))
-            x_codes.append(codes)
-
-        v_scale = keep.tile([P, R], U8, name="v_scale", align_bytes=64)
-        nc.vector.tensor_copy(v_scale[:], vs_table[:].indirect(cand_sb[:]))
-
-        h_ps = [psum.tile([P, S], F32, name="h_ps%d" % j) for j in range(PACK)]
-        for g in range(PASSES):
-            for j in range(PACK):
-                cols = slice(j * P, (j + 1) * P)
-                nc.tensor.matmul_mx(
-                    out=h_ps[j][:],
-                    lhsT=w_codes[g][:, cols].bitcast(FP8X4),
-                    lhsT_scale=w_scale[g][:, cols],
-                    rhs=x_codes[g][:].bitcast(FP8X4),
-                    rhs_scale=x_scale[4 * g :, :],
-                    start=(g == 0),
-                    stop=(g == PASSES - 1),
+            for part in range(PARTS):
+                x_codes[g, part] = keep.tile([P, S // PARTS], U32, name="x_codes%d%d" % (g, part), align_bytes=64)
+                nc.vector.tensor_copy(
+                    x_codes[g, part][:], x_table[g][:].bitcast(U32).indirect(list_part(offs_sb, part))
                 )
 
-        terms = [keep.tile([P, PACK, V], F32, name="terms%d" % d, tag="terms%d" % d) for d in range(2)]
-        for j in range(PACK):
-            h_sb = keep.tile([P, S], F32, name="h_sb%d" % j)
-            nc.scalar.activation(out=h_sb[:], in_=h_ps[j][:], func=ACT.Relu)
+        terms = [keep.tile([P, PACK, V], F32, name="terms%d" % d) for d in range(2)]
+        for lane in range(PACK):
+            cols = slice(lane * P, (lane + 1) * P)
+            h_sb = keep.tile([P, S], F32, name="h_sb%d" % lane)
+            for part in range(PARTS):
+                entries = slice(part * S // PARTS, (part + 1) * S // PARTS)
+                h_ps = psum.tile(
+                    [P, S // PARTS], F32, name="h_ps%d%d" % (lane, part), tag="h_ps%d%d" % (lane % BANK_SETS, part)
+                )
+                for g in range(PASSES):
+                    nc.tensor.matmul_mx(
+                        out=h_ps[:],
+                        lhsT=w_codes[g][:, cols].bitcast(FP8X4),
+                        lhsT_scale=w_scale[g][:, cols],
+                        rhs=x_codes[g, part][:].bitcast(FP8X4),
+                        rhs_scale=x_scale[:, g, entries],
+                        start=(g == 0),
+                        stop=(g == PASSES - 1),
+                    )
+                nc.scalar.activation(out=h_sb[:, entries], in_=h_ps[:], func=ACT.Relu)
             for d in range(2):
-                nc.vector.tensor_tensor(terms[d][:, j, :], h_sb[:].indirect(pos_sb[d][:]), gate_sb[:, d, :], ALU.mult)
-
-        v_codes = keep.tile([P, R], U32, name="v_codes", align_bytes=64)
-        nc.vector.tensor_copy(v_codes[:], v_table[:].bitcast(U32).indirect(cand_sb[:]))
+                nc.vector.tensor_tensor(
+                    terms[d][:, lane, :], h_sb[:].indirect(pos_sb[d][:]), gate_sb[:, d, :], ALU.mult
+                )
 
         z_grouped = []
-        for half in range(HALVES):
-            cols = slice(half * P, (half + 1) * P)
-            grouped = keep.tile([P, P * PACK], BF16, name="z_grouped%d" % half, align_bytes=64)
+        for w in range(WINDOW_TILES):
+            windows = slice(w * P, (w + 1) * P)
+            z_grouped.append(keep.tile([P, P * PACK], BF16, name="z_grouped%d" % w, align_bytes=64))
             nc.vector.tensor_tensor(
-                grouped[:].rearrange("p (c i j) -> p c j i", i=4, j=PACK),
-                terms[0][:, :, cols].rearrange("p j (c i) -> p c j i", i=4),
-                terms[1][:, :, cols].rearrange("p j (c i) -> p c j i", i=4),
+                z_grouped[w][:].rearrange("p (c near lane) -> p c lane near", near=4, lane=PACK),
+                terms[0][:, :, windows].rearrange("p lane (c near) -> p c lane near", near=4),
+                terms[1][:, :, windows].rearrange("p lane (c near) -> p c lane near", near=4),
                 ALU.add,
             )
-            z_grouped.append(grouped)
-        y_ps = []
-        for half in range(HALVES):
-            codes = keep.tile([P, P], U32, name="z_codes%d" % half, align_bytes=64)
-            scale = keep.tile([P, P], U8, name="z_scale%d" % half, align_bytes=64)
-            nc.vector.quantize_mx(out=codes[:].bitcast(FP8X4), scales=scale[:], in_=z_grouped[half][:])
-            y = psum.tile([P, R], F32, name="y_ps%d" % half)
-            nc.tensor.matmul_mx(
-                out=y[:],
-                lhsT=codes[:].bitcast(FP8X4),
-                lhsT_scale=scale[:],
-                rhs=v_codes[:].bitcast(FP8X4),
-                rhs_scale=v_scale[8:, :],
-                start=True,
-                stop=True,
-            )
-            y_ps.append(y)
-        for half in range(HALVES):
-            neg_max = keep.tile([P, 1], F32, name="neg_max%d" % half)
-            nc.vector.tensor_reduce(out=neg_max[:], in_=y_ps[half][:], axis=AXIS.X, op=ALU.max, negate=True)
-            e = keep.tile([P, R], F32, name="e%d" % half)
-            total = keep.tile([P, 1], F32, name="total%d" % half)
-            nc.scalar.activation(out=e[:], in_=y_ps[half][:], func=ACT.Exp, bias=neg_max[:], accum_out=total[:])
-            inv = keep.tile([P, 1], F32, name="inv%d" % half)
-            nc.vector.reciprocal(out=inv[:], in_=total[:])
-            res = keep.tile([P, R], F32, name="res%d" % half)
-            nc.vector.tensor_scalar(out=res[:], in0=e[:], scalar1=inv[:], scalar2=None, op0=ALU.mult)
-            nc.sync.dma_start(out=out[half * P : (half + 1) * P, :], in_=res[:])
+        z_codes = []
+        z_scale = []
+        for w in range(WINDOW_TILES):
+            z_codes.append(keep.tile([P, P], U32, name="z_codes%d" % w, align_bytes=64))
+            z_scale.append(keep.tile([P, P], U8, name="z_scale%d" % w, align_bytes=64))
+            nc.vector.quantize_mx(out=z_codes[w][:].bitcast(FP8X4), scales=z_scale[w][:], in_=z_grouped[w][:])
+
+        y_ps = [psum.tile([P, R], F32, name="y_ps%d" % w) for w in range(WINDOW_TILES)]
+        for part in range(PARTS):
+            entries = slice(part * R // PARTS, (part + 1) * R // PARTS)
+            v_codes = keep.tile([P, R // PARTS], U32, name="v_codes%d" % part, align_bytes=64)
+            nc.vector.tensor_copy(v_codes[:], v_table[:].bitcast(U32).indirect(list_part(cand_sb, part)))
+            for w in range(WINDOW_TILES):
+                nc.tensor.matmul_mx(
+                    out=y_ps[w][:, entries],
+                    lhsT=z_codes[w][:].bitcast(FP8X4),
+                    lhsT_scale=z_scale[w][:],
+                    rhs=v_codes[:].bitcast(FP8X4),
+                    rhs_scale=v_scale[:, entries],
+                    start=True,
+                    stop=True,
+                )
+
+        for w in range(WINDOW_TILES):
+            neg_max = keep.tile([P, 1], F32, name="neg_max%d" % w)
+            nc.vector.tensor_reduce(out=neg_max[:], in_=y_ps[w][:], axis=AXIS.X, op=ALU.max, negate=True)
+            exps = keep.tile([P, R], F32, name="exps%d" % w)
+            total = keep.tile([P, 1], F32, name="total%d" % w)
+            nc.scalar.activation(out=exps[:], in_=y_ps[w][:], func=ACT.Exp, bias=neg_max[:], accum_out=total[:])
+            inv_total = keep.tile([P, 1], F32, name="inv_total%d" % w)
+            nc.vector.reciprocal(out=inv_total[:], in_=total[:])
+            probs = keep.tile([P, R], F32, name="probs%d" % w)
+            nc.vector.tensor_scalar(out=probs[:], in0=exps[:], scalar1=inv_total[:], scalar2=None, op0=ALU.mult)
+            nc.sync.dma_start(out=out[w * P : (w + 1) * P, :], in_=probs[:])

@@ -1,6 +1,7 @@
 from contextlib import ExitStack
 
 import concourse.mybir as mybir
+from concourse.masks import make_identity
 
 F32 = mybir.dt.float32
 BF16 = mybir.dt.bfloat16
@@ -21,8 +22,10 @@ QUADRANT = 32
 SPREAD = 8
 PASSES = K // (P * PACK)
 WINDOW_TILES = V // P
+ROW_TILES = H // P
+HALF = H // 2
 PARTS = 2
-BANK_SETS = 2
+NEAR = 4
 HEAD = T // 4
 FLOPS = 2 * K * H * S + 2 * H * V * R
 
@@ -38,40 +41,64 @@ def tile_picked_zcbow_relu_p_kernel(
         offs_sb = keep.tile([P, S // LIST], U16, name="offs_sb")
         pos_sb = [keep.tile([P, V // LIST], U16, name="pos_sb%d" % d) for d in range(2)]
         cand_sb = keep.tile([P, R // LIST], U16, name="cand_sb")
-        w_raw = [keep.tile([P, PACK, H], F32, name="w_raw%d" % g) for g in range(PASSES)]
-        x_table = [keep.tile([P, T], I32, name="x_table%d" % g) for g in range(PASSES)]
-        v_table = keep.tile([P, G], I32, name="v_table")
-        xs_table = keep.tile([P, PASSES, T], U8, name="xs_table")
-        vs_table = keep.tile([P, G], U8, name="vs_table")
+        x_table = [keep.tile([P, T], I32, name="x_table%d" % g, tag="table%d" % g, align_bytes=64) for g in range(PASSES)]
+        xs_table = keep.tile([P, PASSES, T], U8, name="xs_table", tag="after_x_scales", align_bytes=64)
+        vs_table = keep.tile([P, G], U8, name="vs_table", tag="after_v_scales")
         x_scale = keep.tile([P, PASSES, S], U8, name="x_scale", align_bytes=64)
-        v_scale = keep.tile([P, R], U8, name="v_scale", align_bytes=64)
-        gate_sb = keep.tile([P, 2, V], F32, name="gate_sb")
 
         nc.gpsimd.memset(xs_table[:, 1, :].bitcast(I32), 0)
         nc.vector.memset(xs_table[:, 0, :].bitcast(I32), 0)
         nc.vector.memset(vs_table[:].bitcast(I32), 0)
         nc.vector.memset(x_scale[:].bitcast(I32), 0)
-        nc.vector.memset(v_scale[:].bitcast(I32), 0)
 
-        def load_w(g):
-            rows = w1[g * P * PACK : (g + 1) * P * PACK, :]
-            nc.sync.dma_start(out=w_raw[g][:], in_=rows.rearrange("(p j) c -> p j c", j=PACK))
+        def load_w(g, first, count, tag):
+            raw = keep.tile([P, PACK, count], F32, name="w_raw%d%d" % (g, first), tag=tag, align_bytes=64)
+            rows = w1[g * P * PACK : (g + 1) * P * PACK, first : first + count]
+            nc.sync.dma_start(out=raw[:], in_=rows.rearrange("(p j) c -> p j c", j=PACK))
+            return raw
 
         def words(table):
             return table.rearrange("p n j -> p (n j)").bitcast(I32)
 
-        def list_part(list_sb, part):
-            columns = list_sb.shape[1] // PARTS
+        def list_part(list_sb, part, parts):
+            columns = list_sb.shape[1] // parts
             return list_sb[:, part * columns : (part + 1) * columns]
 
-        nc.sync.dma_start(out=x_table[0][:, :HEAD], in_=words(x_words[0])[:, :HEAD])
+        def group_w(engine_copy, grouped, columns, first, count):
+            engine_copy(
+                out=grouped.rearrange("p (u m e j) -> p m j u e", u=count, e=2, j=PACK),
+                in_=columns.rearrange("p j (m u e) -> p m j u e", u=2, e=2)[:, :, :, first : first + count, :],
+            )
+
+        def grouped_tile(name, row_tiles):
+            return keep.tile([P, row_tiles * P * PACK], BF16, name=name, align_bytes=64)
+
+        w_codes = {}
+        w_scale = {}
+
+        def quantise_w(grouped, g, first_tile):
+            count = grouped.shape[1] // PACK
+            name = "%d%d" % (g, first_tile)
+            codes = keep.tile([P, count], U32, name="w_codes" + name, tag="w_codes" + name, align_bytes=64)
+            scale = keep.tile([P, count], U8, name="w_scale" + name, align_bytes=64)
+            nc.vector.quantize_mx(out=codes[:].bitcast(FP8X4), scales=scale[:], in_=grouped[:])
+            for n in range(count // P):
+                w_codes[g, first_tile + n] = codes[:, n * P : (n + 1) * P]
+                w_scale[g, first_tile + n] = scale[:, n * P : (n + 1) * P]
+
+        def load_x(g, first, last):
+            nc.sync.dma_start(out=x_table[g][:, first:last], in_=words(x_words[g])[:, first:last])
+
+        load_x(0, 0, HEAD)
         nc.sync.dma_start(offs_sb[:], offs)
-        nc.sync.dma_start(cand_sb[:], cand)
         nc.sync.dma_start(out=xs_table[0:P:SPREAD].bitcast(I32), in_=x_scales.rearrange("g n c -> n g c").bitcast(I32))
-        load_w(0)
+        w_first = load_w(0, 0, H, "w_first")
+        nc.sync.dma_start(cand_sb[:], cand)
         nc.sync.dma_start(out=vs_table[SPREAD // 2 : P : SPREAD].bitcast(I32), in_=v_scales[0].bitcast(I32))
-        load_w(1)
-        nc.sync.dma_start(out=x_table[0][:, HEAD:], in_=words(x_words[0])[:, HEAD:])
+        load_x(0, HEAD, T)
+        nc.sync.dma_start(pos_sb[0][:], pos1)
+        nc.sync.dma_start(pos_sb[1][:], pos2)
+        load_x(1, 0, T)
 
         xs_picked = keep.tile([P, PASSES, S], U8, name="xs_picked")
         for g in range(PASSES):
@@ -80,97 +107,149 @@ def tile_picked_zcbow_relu_p_kernel(
             nc.sync.dma_start(
                 out=x_scale[r:P:QUADRANT].bitcast(I32), in_=xs_picked[SPREAD * r : P : QUADRANT].bitcast(I32)
             )
-        nc.sync.dma_start(out=x_table[1][:], in_=words(x_words[1]))
-        nc.sync.dma_start(pos_sb[0][:], pos1)
-        nc.sync.dma_start(pos_sb[1][:], pos2)
+        w_low = load_w(1, 0, HALF, "after_x_scales")
+        w_high = load_w(1, HALF, HALF, "w_high")
+        gate_sb = keep.tile([P, 2, V], F32, name="gate_sb")
         nc.sync.dma_start(out=gate_sb[:], in_=gate.rearrange("d p v -> p d v"))
-        nc.sync.dma_start(out=v_table[:], in_=words(v_words[0]))
-        vs_picked = keep.tile([P, R], U8, name="vs_picked")
-        nc.vector.tensor_copy(vs_picked[:], vs_table[:].indirect(cand_sb[:]))
-        for r in range(4):
-            nc.sync.dma_start(
-                out=v_scale[r:P:QUADRANT].bitcast(I32),
-                in_=vs_picked[SPREAD * r + SPREAD // 2 : P : QUADRANT].bitcast(I32),
-            )
+        x_codes = []
 
-        w_codes = []
-        w_scale = []
-        for g in range(PASSES):
-            w_grouped = keep.tile([P, H * PACK], BF16, name="w_grouped%d" % g, align_bytes=64)
-            nc.scalar.activation(
-                out=w_grouped[:].rearrange("p (lane m j) -> p m j lane", lane=PACK, j=PACK),
-                in_=w_raw[g][:].rearrange("p j (m lane) -> p m j lane", lane=PACK),
-                func=ACT.Copy,
-            )
-            w_codes.append(keep.tile([P, H], U32, name="w_codes%d" % g, align_bytes=64))
-            w_scale.append(keep.tile([P, H], U8, name="w_scale%d" % g, align_bytes=64))
-            nc.vector.quantize_mx(out=w_codes[g][:].bitcast(FP8X4), scales=w_scale[g][:], in_=w_grouped[:])
-
-        x_codes = {}
-        for g in range(PASSES):
-            for part in range(PARTS):
-                x_codes[g, part] = keep.tile([P, S // PARTS], U32, name="x_codes%d%d" % (g, part), align_bytes=64)
-                nc.vector.tensor_copy(
-                    x_codes[g, part][:], x_table[g][:].bitcast(U32).indirect(list_part(offs_sb, part))
-                )
-
-        terms = [keep.tile([P, PACK, V], F32, name="terms%d" % d) for d in range(2)]
-        for lane in range(PACK):
-            cols = slice(lane * P, (lane + 1) * P)
-            h_sb = keep.tile([P, S], F32, name="h_sb%d" % lane)
+        def gather_x(g):
+            x_codes.append(keep.tile([P, S], U32, name="x_codes%d" % g, align_bytes=64))
             for part in range(PARTS):
                 entries = slice(part * S // PARTS, (part + 1) * S // PARTS)
-                h_ps = psum.tile(
-                    [P, S // PARTS], F32, name="h_ps%d%d" % (lane, part), tag="h_ps%d%d" % (lane % BANK_SETS, part)
+                nc.vector.tensor_copy(
+                    x_codes[g][:, entries], x_table[g][:].bitcast(U32).indirect(list_part(offs_sb, part, PARTS))
                 )
+
+        vs_picked = keep.tile([P, R], U8, name="vs_picked")
+        nc.vector.tensor_copy(vs_picked[:], vs_table[:].indirect(cand_sb[:]))
+        gather_x(0)
+
+        grouped = grouped_tile("grouped_first", ROW_TILES)
+        for half in range(2):
+            places = slice(half * HALF * PACK, (half + 1) * HALF * PACK)
+            group_w(nc.scalar.copy, grouped[:, places], w_first[:, :, half * HALF : (half + 1) * HALF], 0, 2)
+        quantise_w(grouped, 0, 0)
+
+        ident = keep.tile([P, P], F32, name="ident", tag="after_v_scales")
+        make_identity(nc, ident[:])
+
+        gather_x(1)
+        v_table = keep.tile([P, G], I32, name="v_table", tag="table0", align_bytes=64)
+        nc.sync.dma_start(out=v_table[:], in_=words(v_words[0]))
+
+        grouped = [grouped_tile("grouped_low%d" % u, 1) for u in range(2)]
+        for u, engine_copy in enumerate((nc.vector.tensor_copy, nc.scalar.copy)):
+            group_w(engine_copy, grouped[u][:], w_low[:], u, 1)
+        for u in range(2):
+            quantise_w(grouped[u], 1, u)
+        grouped = grouped_tile("grouped_high", 2)
+        group_w(nc.vector.tensor_copy, grouped[:], w_high[:], 0, 2)
+        quantise_w(grouped, 1, 2)
+
+        def first_product(tile_no, parts, banks):
+            sums = []
+            for part in range(parts):
+                entries = slice(part * S // parts, (part + 1) * S // parts)
+                h_ps = psum.tile([P, S // parts], F32, name="h_ps%d%d" % (tile_no, part), tag=banks[part])
                 for g in range(PASSES):
                     nc.tensor.matmul_mx(
                         out=h_ps[:],
-                        lhsT=w_codes[g][:, cols].bitcast(FP8X4),
-                        lhsT_scale=w_scale[g][:, cols],
-                        rhs=x_codes[g, part][:].bitcast(FP8X4),
+                        lhsT=w_codes[g, tile_no].bitcast(FP8X4),
+                        lhsT_scale=w_scale[g, tile_no],
+                        rhs=x_codes[g][:, entries].bitcast(FP8X4),
                         rhs_scale=x_scale[:, g, entries],
                         start=(g == 0),
                         stop=(g == PASSES - 1),
                     )
+                sums.append(h_ps)
+            return sums
+
+        def relu_out(tile_no, sums, tag):
+            h_sb = keep.tile([P, S], F32, name="h_sb%d" % tile_no, tag=tag, align_bytes=64)
+            for part, h_ps in enumerate(sums):
+                entries = slice(part * S // len(sums), (part + 1) * S // len(sums))
                 nc.scalar.activation(out=h_sb[:, entries], in_=h_ps[:], func=ACT.Relu)
+            return h_sb
+
+        def gather_term(term, h_tile, d, part, parts):
+            count = V // parts
+            nc.vector.tensor_tensor(
+                term,
+                h_tile[:].indirect(list_part(pos_sb[d], part, parts)),
+                gate_sb[:, d, part * count : (part + 1) * count],
+                ALU.mult,
+            )
+
+        def add_turned(z_ps, terms):
             for d in range(2):
-                nc.vector.tensor_tensor(
-                    terms[d][:, lane, :], h_sb[:].indirect(pos_sb[d][:]), gate_sb[:, d, :], ALU.mult
-                )
+                nc.tensor.matmul(z_ps, lhsT=terms[d], rhs=ident[:], is_transpose=True, start=(d == 0), stop=(d == 1))
+
+        h_sb = [relu_out(0, first_product(0, PARTS, ["bank_y0", "bank_y1"]), "h_sb0")]
+        for tile_no, bank in ((1, "bank_a"), (2, "bank_y0"), (3, "bank_y1")):
+            h_sb.append(relu_out(tile_no, first_product(tile_no, 1, [bank]), "h_sb%d" % tile_no))
+
+        v_scale = x_scale[4:P, 0, :]
+        for r in range(4):
+            nc.sync.dma_start(
+                out=x_scale[4 + r : P : QUADRANT, 0, :].bitcast(I32),
+                in_=vs_picked[SPREAD * r + SPREAD // 2 : P : QUADRANT].bitcast(I32),
+            )
+
+        z_rows = [keep.tile([P, 2, 2, P], BF16, name="z_rows%d" % w) for w in range(WINDOW_TILES)]
+        back_ps = [psum.tile([P, 2, P], F32, name="back_ps%d" % w) for w in range(WINDOW_TILES)]
+
+        def turn_back(w, u):
+            pairs = z_rows[w][:, u].rearrange("t half c -> t (half c)").bitcast(F32)
+            nc.tensor.transpose(back_ps[w][:, u, :], pairs, ident[:])
+
+        terms = keep.tile([P, ROW_TILES - 1, 2, V], F32, name="terms", tag="w_high", align_bytes=64)
+        for tile_no in range(ROW_TILES - 1):
+            for d in range(2):
+                gather_term(terms[:, tile_no, d, :], h_sb[tile_no], d, 0, 1)
+        z_ps = [psum.tile([P, 3, P], F32, name="z_ps%d" % w, tag=["bank_a", "bank_z1"][w]) for w in range(WINDOW_TILES)]
+        for w in range(WINDOW_TILES):
+            for tile_no in range(2):
+                add_turned(z_ps[w][:, tile_no, :], [terms[:, tile_no, d, w * P : (w + 1) * P] for d in range(2)])
+            nc.scalar.copy(out=z_rows[w][:, :, 0, :], in_=z_ps[w][:, 0:2, :])
+        for w in range(WINDOW_TILES):
+            add_turned(z_ps[w][:, 2, :], [terms[:, 2, d, w * P : (w + 1) * P] for d in range(2)])
+            nc.scalar.copy(out=z_rows[w][:, 0, 1, :], in_=z_ps[w][:, 2, :])
+            turn_back(w, 0)
 
         z_grouped = []
         for w in range(WINDOW_TILES):
-            windows = slice(w * P, (w + 1) * P)
+            last_terms = keep.tile([P, 2, P], F32, name="last_terms%d" % w)
+            for d in range(2):
+                gather_term(last_terms[:, d, :], h_sb[3], d, w, WINDOW_TILES)
+            last_ps = psum.tile([P, P], F32, name="last_ps%d" % w)
+            add_turned(last_ps[:], [last_terms[:, d, :] for d in range(2)])
+            nc.scalar.copy(out=z_rows[w][:, 1, 1, :], in_=last_ps[:])
+            turn_back(w, 1)
             z_grouped.append(keep.tile([P, P * PACK], BF16, name="z_grouped%d" % w, align_bytes=64))
-            nc.vector.tensor_tensor(
-                z_grouped[w][:].rearrange("p (c near lane) -> p c lane near", near=4, lane=PACK),
-                terms[0][:, :, windows].rearrange("p lane (c near) -> p c lane near", near=4),
-                terms[1][:, :, windows].rearrange("p lane (c near) -> p c lane near", near=4),
-                ALU.add,
+            nc.scalar.copy(
+                out=z_grouped[w][:].bitcast(F32).rearrange("p (t u) -> p t u", u=2),
+                in_=back_ps[w][:].rearrange("p u t -> p t u"),
             )
-        z_codes = []
-        z_scale = []
-        for w in range(WINDOW_TILES):
-            z_codes.append(keep.tile([P, P], U32, name="z_codes%d" % w, align_bytes=64))
-            z_scale.append(keep.tile([P, P], U8, name="z_scale%d" % w, align_bytes=64))
-            nc.vector.quantize_mx(out=z_codes[w][:].bitcast(FP8X4), scales=z_scale[w][:], in_=z_grouped[w][:])
 
-        y_ps = [psum.tile([P, R], F32, name="y_ps%d" % w) for w in range(WINDOW_TILES)]
-        for part in range(PARTS):
-            entries = slice(part * R // PARTS, (part + 1) * R // PARTS)
-            v_codes = keep.tile([P, R // PARTS], U32, name="v_codes%d" % part, align_bytes=64)
-            nc.vector.tensor_copy(v_codes[:], v_table[:].bitcast(U32).indirect(list_part(cand_sb, part)))
-            for w in range(WINDOW_TILES):
-                nc.tensor.matmul_mx(
-                    out=y_ps[w][:, entries],
-                    lhsT=z_codes[w][:].bitcast(FP8X4),
-                    lhsT_scale=z_scale[w][:],
-                    rhs=v_codes[:].bitcast(FP8X4),
-                    rhs_scale=v_scale[:, entries],
-                    start=True,
-                    stop=True,
-                )
+        v_codes = keep.tile([P, R], U32, name="v_codes", tag="h_sb3", align_bytes=64)
+        nc.vector.tensor_copy(v_codes[:], v_table[:].bitcast(U32).indirect(cand_sb[:]))
+
+        y_ps = []
+        for w in range(WINDOW_TILES):
+            z_codes = keep.tile([P, P], U32, name="z_codes%d" % w, align_bytes=64)
+            z_scale = keep.tile([P, P], U8, name="z_scale%d" % w, align_bytes=64)
+            nc.vector.quantize_mx(out=z_codes[:].bitcast(FP8X4), scales=z_scale[:], in_=z_grouped[w][:])
+            y_ps.append(psum.tile([P, R], F32, name="y_ps%d" % w, tag="bank_y%d" % w))
+            nc.tensor.matmul_mx(
+                out=y_ps[w][:],
+                lhsT=z_codes[:].bitcast(FP8X4),
+                lhsT_scale=z_scale[:],
+                rhs=v_codes[:].bitcast(FP8X4),
+                rhs_scale=v_scale,
+                start=True,
+                stop=True,
+            )
 
         for w in range(WINDOW_TILES):
             neg_max = keep.tile([P, 1], F32, name="neg_max%d" % w)

@@ -23,9 +23,8 @@ SPREAD = 8
 PASSES = K // (P * PACK)
 WINDOW_TILES = V // P
 ROW_TILES = H // P
-HALF = H // 2
 PARTS = 2
-NEAR = 4
+HALF = H // 2
 HEAD = T // 4
 FLOPS = 2 * K * H * S + 2 * H * V * R
 
@@ -42,20 +41,18 @@ def tile_picked_zcbow_relu_p_kernel(
         pos_sb = [keep.tile([P, V // LIST], U16, name="pos_sb%d" % d) for d in range(2)]
         cand_sb = keep.tile([P, R // LIST], U16, name="cand_sb")
         x_table = [keep.tile([P, T], I32, name="x_table%d" % g, tag="table%d" % g, align_bytes=64) for g in range(PASSES)]
-        xs_table = keep.tile([P, PASSES, T], U8, name="xs_table", tag="after_x_scales", align_bytes=64)
-        vs_table = keep.tile([P, G], U8, name="vs_table", tag="after_v_scales")
+        xs_table = keep.tile([P, PASSES, T], U8, name="xs_table", align_bytes=64)
+        vs_table = keep.tile([P, G], U8, name="vs_table")
         x_scale = keep.tile([P, PASSES, S], U8, name="x_scale", align_bytes=64)
+        ident = keep.tile([P, P], F32, name="ident")
+        gate_rows = keep.tile([P, P], F32, name="gate_rows")
 
-        nc.gpsimd.memset(xs_table[:, 1, :].bitcast(I32), 0)
-        nc.vector.memset(xs_table[:, 0, :].bitcast(I32), 0)
+        nc.vector.memset(xs_table[:].bitcast(I32), 0)
         nc.vector.memset(vs_table[:].bitcast(I32), 0)
+        nc.vector.memset(ident[:], 0.0)
+        nc.vector.memset(gate_rows[:], 0.0)
         nc.vector.memset(x_scale[:].bitcast(I32), 0)
-
-        def load_w(g, first, count, tag):
-            raw = keep.tile([P, PACK, count], F32, name="w_raw%d%d" % (g, first), tag=tag, align_bytes=64)
-            rows = w1[g * P * PACK : (g + 1) * P * PACK, first : first + count]
-            nc.sync.dma_start(out=raw[:], in_=rows.rearrange("(p j) c -> p j c", j=PACK))
-            return raw
+        make_identity(nc, ident[:], nomemset=True)
 
         def words(table):
             return table.rearrange("p n j -> p (n j)").bitcast(I32)
@@ -64,14 +61,17 @@ def tile_picked_zcbow_relu_p_kernel(
             columns = list_sb.shape[1] // parts
             return list_sb[:, part * columns : (part + 1) * columns]
 
+        def w_rows(g):
+            return w1[g * P * PACK : (g + 1) * P * PACK, :].rearrange("(p j) c -> p j c", j=PACK)
+
         def group_w(engine_copy, grouped, columns, first, count):
             engine_copy(
                 out=grouped.rearrange("p (u m e j) -> p m j u e", u=count, e=2, j=PACK),
                 in_=columns.rearrange("p j (m u e) -> p m j u e", u=2, e=2)[:, :, :, first : first + count, :],
             )
 
-        def grouped_tile(name, row_tiles):
-            return keep.tile([P, row_tiles * P * PACK], BF16, name=name, align_bytes=64)
+        def grouped_tile(name, row_tiles, tag):
+            return keep.tile([P, row_tiles * P * PACK], BF16, name=name, tag=tag, align_bytes=64)
 
         w_codes = {}
         w_scale = {}
@@ -86,19 +86,18 @@ def tile_picked_zcbow_relu_p_kernel(
                 w_codes[g, first_tile + n] = codes[:, n * P : (n + 1) * P]
                 w_scale[g, first_tile + n] = scale[:, n * P : (n + 1) * P]
 
-        def load_x(g, first, last):
-            nc.sync.dma_start(out=x_table[g][:, first:last], in_=words(x_words[g])[:, first:last])
-
-        load_x(0, 0, HEAD)
+        w_first = keep.tile([P, PACK, H], F32, name="w_first")
+        w_low = keep.tile([P, PACK, HALF], F32, name="w_low")
+        w_high = keep.tile([P, PACK, HALF], F32, name="w_high", tag="w_high", align_bytes=64)
+        nc.sync.dma_start(out=x_table[0][:, 0:HEAD], in_=words(x_words[0])[:, 0:HEAD])
         nc.sync.dma_start(offs_sb[:], offs)
-        nc.sync.dma_start(out=xs_table[0:P:SPREAD].bitcast(I32), in_=x_scales.rearrange("g n c -> n g c").bitcast(I32))
-        w_first = load_w(0, 0, H, "w_first")
         nc.sync.dma_start(cand_sb[:], cand)
+        nc.sync.dma_start(out=xs_table[0:P:SPREAD].bitcast(I32), in_=x_scales.rearrange("g n c -> n g c").bitcast(I32))
+        nc.sync.dma_start(out=w_first[:], in_=w_rows(0))
         nc.sync.dma_start(out=vs_table[SPREAD // 2 : P : SPREAD].bitcast(I32), in_=v_scales[0].bitcast(I32))
-        load_x(0, HEAD, T)
-        nc.sync.dma_start(pos_sb[0][:], pos1)
-        nc.sync.dma_start(pos_sb[1][:], pos2)
-        load_x(1, 0, T)
+        nc.sync.dma_start(out=x_table[0][:, HEAD:T], in_=words(x_words[0])[:, HEAD:T])
+        nc.sync.dma_start(out=gate_rows[0:4, :], in_=gate[:, 0, :].rearrange("d (w c) -> d w c", c=P))
+        nc.sync.dma_start(out=w_low[:], in_=w_rows(1)[:, :, 0:HALF])
 
         xs_picked = keep.tile([P, PASSES, S], U8, name="xs_picked")
         for g in range(PASSES):
@@ -107,45 +106,47 @@ def tile_picked_zcbow_relu_p_kernel(
             nc.sync.dma_start(
                 out=x_scale[r:P:QUADRANT].bitcast(I32), in_=xs_picked[SPREAD * r : P : QUADRANT].bitcast(I32)
             )
-        w_low = load_w(1, 0, HALF, "after_x_scales")
-        w_high = load_w(1, HALF, HALF, "w_high")
-        gate_sb = keep.tile([P, 2, V], F32, name="gate_sb")
-        nc.sync.dma_start(out=gate_sb[:], in_=gate.rearrange("d p v -> p d v"))
-        x_codes = []
-
-        def gather_x(g):
-            x_codes.append(keep.tile([P, S], U32, name="x_codes%d" % g, align_bytes=64))
-            for part in range(PARTS):
-                entries = slice(part * S // PARTS, (part + 1) * S // PARTS)
-                nc.vector.tensor_copy(
-                    x_codes[g][:, entries], x_table[g][:].bitcast(U32).indirect(list_part(offs_sb, part, PARTS))
-                )
+        nc.sync.dma_start(out=x_table[1][:], in_=words(x_words[1]))
+        nc.sync.dma_start(out=w_high[:], in_=w_rows(1)[:, :, HALF:H])
+        nc.sync.dma_start(pos_sb[0][:], pos1)
+        nc.sync.dma_start(pos_sb[1][:], pos2)
 
         vs_picked = keep.tile([P, R], U8, name="vs_picked")
         nc.vector.tensor_copy(vs_picked[:], vs_table[:].indirect(cand_sb[:]))
-        gather_x(0)
 
-        grouped = grouped_tile("grouped_first", ROW_TILES)
+        x_codes = []
+
+        def gather_x(g, parts):
+            x_codes.append(keep.tile([P, S], U32, name="x_codes%d" % g, align_bytes=64))
+            for part in range(parts):
+                entries = slice(part * S // parts, (part + 1) * S // parts)
+                nc.vector.tensor_copy(
+                    x_codes[g][:, entries], x_table[g][:].bitcast(U32).indirect(list_part(offs_sb, part, parts))
+                )
+
+        grouped = [grouped_tile("grouped_first%d" % half, 2, "grouped_first%d" % half) for half in range(2)]
         for half in range(2):
-            places = slice(half * HALF * PACK, (half + 1) * HALF * PACK)
-            group_w(nc.scalar.copy, grouped[:, places], w_first[:, :, half * HALF : (half + 1) * HALF], 0, 2)
-        quantise_w(grouped, 0, 0)
-
-        ident = keep.tile([P, P], F32, name="ident", tag="after_v_scales")
-        make_identity(nc, ident[:])
-
-        gather_x(1)
+            group_w(nc.scalar.copy, grouped[half][:], w_first[:, :, half * HALF : (half + 1) * HALF], 0, 2)
+        quantise_w(grouped[0], 0, 0)
+        gather_x(0, 1)
+        quantise_w(grouped[1], 0, 2)
         v_table = keep.tile([P, G], I32, name="v_table", tag="table0", align_bytes=64)
         nc.sync.dma_start(out=v_table[:], in_=words(v_words[0]))
 
-        grouped = [grouped_tile("grouped_low%d" % u, 1) for u in range(2)]
-        for u, engine_copy in enumerate((nc.vector.tensor_copy, nc.scalar.copy)):
-            group_w(engine_copy, grouped[u][:], w_low[:], u, 1)
-        for u in range(2):
-            quantise_w(grouped[u], 1, u)
-        grouped = grouped_tile("grouped_high", 2)
-        group_w(nc.vector.tensor_copy, grouped[:], w_high[:], 0, 2)
-        quantise_w(grouped, 1, 2)
+        column_ps = psum.tile([P, P], F32, name="column_ps", tag="bank_back0")
+        nc.tensor.transpose(column_ps[:], gate_rows[:], ident[:])
+        gate_column = keep.tile([P, 4], F32, name="gate_column")
+        nc.scalar.copy(out=gate_column[:], in_=column_ps[:, 0:4])
+        gate_ps = psum.tile([P, 4, P], F32, name="gate_ps", tag="bank_back1")
+        for c in range(4):
+            nc.tensor.transpose(gate_ps[:, c, :], gate_column[:, c : c + 1].to_broadcast([P, P]), ident[:])
+        gate_sb = keep.tile([P, 2, V], F32, name="gate_sb")
+        nc.scalar.copy(out=gate_sb[:].rearrange("p d v -> p (d v)"), in_=gate_ps[:].rearrange("p c t -> p (c t)"))
+
+        grouped = grouped_tile("grouped_low", 2, "grouped_low")
+        group_w(nc.scalar.copy, grouped[:], w_low[:], 0, 2)
+        quantise_w(grouped, 1, 0)
+        gather_x(1, PARTS)
 
         def first_product(tile_no, parts, banks):
             sums = []
@@ -166,11 +167,11 @@ def tile_picked_zcbow_relu_p_kernel(
             return sums
 
         def relu_out(tile_no, sums, tag):
-            h_sb = keep.tile([P, S], F32, name="h_sb%d" % tile_no, tag=tag, align_bytes=64)
+            h_tile = keep.tile([P, S], F32, name="h_sb%d" % tile_no, tag=tag, align_bytes=64)
             for part, h_ps in enumerate(sums):
                 entries = slice(part * S // len(sums), (part + 1) * S // len(sums))
-                nc.scalar.activation(out=h_sb[:, entries], in_=h_ps[:], func=ACT.Relu)
-            return h_sb
+                nc.scalar.activation(out=h_tile[:, entries], in_=h_ps[:], func=ACT.Relu)
+            return h_tile
 
         def gather_term(term, h_tile, d, part, parts):
             count = V // parts
@@ -185,9 +186,15 @@ def tile_picked_zcbow_relu_p_kernel(
             for d in range(2):
                 nc.tensor.matmul(z_ps, lhsT=terms[d], rhs=ident[:], is_transpose=True, start=(d == 0), stop=(d == 1))
 
-        h_sb = [relu_out(0, first_product(0, PARTS, ["bank_y0", "bank_y1"]), "h_sb0")]
-        for tile_no, bank in ((1, "bank_a"), (2, "bank_y0"), (3, "bank_y1")):
-            h_sb.append(relu_out(tile_no, first_product(tile_no, 1, [bank]), "h_sb%d" % tile_no))
+        h_sb = [relu_out(0, first_product(0, PARTS, ["bank_z0", "bank_z1"]), "h_sb0")]
+        sums = first_product(1, 1, ["bank_last0"])
+        for u, engine_copy, tag in ((0, nc.vector.tensor_copy, "grouped2"), (1, nc.scalar.copy, "w_codes10")):
+            grouped = grouped_tile("grouped_high%d" % u, 1, tag)
+            group_w(engine_copy, grouped[:], w_high[:], u, 1)
+            quantise_w(grouped, 1, 2 + u)
+        h_sb.append(relu_out(1, sums, "w_high"))
+        h_sb.append(relu_out(2, first_product(2, 1, ["bank_last1"]), "h_sb2"))
+        h_sb.append(relu_out(3, first_product(3, 1, ["bank_y0"]), "h_sb3"))
 
         v_scale = x_scale[4:P, 0, :]
         for r in range(4):
@@ -197,23 +204,24 @@ def tile_picked_zcbow_relu_p_kernel(
             )
 
         z_rows = [keep.tile([P, 2, 2, P], BF16, name="z_rows%d" % w) for w in range(WINDOW_TILES)]
-        back_ps = [psum.tile([P, 2, P], F32, name="back_ps%d" % w) for w in range(WINDOW_TILES)]
+        back_ps = [psum.tile([P, 2, P], F32, name="back_ps%d" % w, tag="bank_back%d" % w) for w in range(WINDOW_TILES)]
 
         def turn_back(w, u):
             pairs = z_rows[w][:, u].rearrange("t half c -> t (half c)").bitcast(F32)
             nc.tensor.transpose(back_ps[w][:, u, :], pairs, ident[:])
 
-        terms = keep.tile([P, ROW_TILES - 1, 2, V], F32, name="terms", tag="w_high", align_bytes=64)
-        for tile_no in range(ROW_TILES - 1):
+        terms = []
+        for tile_no, tag in enumerate(("terms0", "terms1", "terms2")):
+            terms.append(keep.tile([P, 2, V], F32, name="terms%d" % tile_no, tag=tag, align_bytes=64))
             for d in range(2):
-                gather_term(terms[:, tile_no, d, :], h_sb[tile_no], d, 0, 1)
-        z_ps = [psum.tile([P, 3, P], F32, name="z_ps%d" % w, tag=["bank_a", "bank_z1"][w]) for w in range(WINDOW_TILES)]
+                gather_term(terms[tile_no][:, d, :], h_sb[tile_no], d, 0, 1)
+        z_ps = [psum.tile([P, 3, P], F32, name="z_ps%d" % w, tag="bank_z%d" % w) for w in range(WINDOW_TILES)]
         for w in range(WINDOW_TILES):
             for tile_no in range(2):
-                add_turned(z_ps[w][:, tile_no, :], [terms[:, tile_no, d, w * P : (w + 1) * P] for d in range(2)])
+                add_turned(z_ps[w][:, tile_no, :], [terms[tile_no][:, d, w * P : (w + 1) * P] for d in range(2)])
             nc.scalar.copy(out=z_rows[w][:, :, 0, :], in_=z_ps[w][:, 0:2, :])
         for w in range(WINDOW_TILES):
-            add_turned(z_ps[w][:, 2, :], [terms[:, 2, d, w * P : (w + 1) * P] for d in range(2)])
+            add_turned(z_ps[w][:, 2, :], [terms[2][:, d, w * P : (w + 1) * P] for d in range(2)])
             nc.scalar.copy(out=z_rows[w][:, 0, 1, :], in_=z_ps[w][:, 2, :])
             turn_back(w, 0)
 
@@ -222,7 +230,7 @@ def tile_picked_zcbow_relu_p_kernel(
             last_terms = keep.tile([P, 2, P], F32, name="last_terms%d" % w)
             for d in range(2):
                 gather_term(last_terms[:, d, :], h_sb[3], d, w, WINDOW_TILES)
-            last_ps = psum.tile([P, P], F32, name="last_ps%d" % w)
+            last_ps = psum.tile([P, P], F32, name="last_ps%d" % w, tag="bank_last%d" % w)
             add_turned(last_ps[:], [last_terms[:, d, :] for d in range(2)])
             nc.scalar.copy(out=z_rows[w][:, 1, 1, :], in_=last_ps[:])
             turn_back(w, 1)

@@ -81,7 +81,7 @@ def tile_picked_zcbow_relu_p_kernel(
             name = "%d%d" % (g, first_tile)
             codes = keep.tile([P, count], U32, name="w_codes" + name, tag="w_codes" + name, align_bytes=64)
             scale = keep.tile([P, count], U8, name="w_scale" + name, align_bytes=64)
-            nc.vector.quantize_mx(out=codes[:].bitcast(FP8X4), scales=scale[:], in_=grouped[:])
+            nc.vector.quantize_mx(out=codes[:].bitcast(FP8X4), scales=scale[:], in_=grouped)
             for n in range(count // P):
                 w_codes[g, first_tile + n] = codes[:, n * P : (n + 1) * P]
                 w_scale[g, first_tile + n] = scale[:, n * P : (n + 1) * P]
@@ -127,9 +127,9 @@ def tile_picked_zcbow_relu_p_kernel(
         grouped = [grouped_tile("grouped_first%d" % half, 2, "grouped_first%d" % half) for half in range(2)]
         for half in range(2):
             group_w(nc.scalar.copy, grouped[half][:], w_first[:, :, half * HALF : (half + 1) * HALF], 0, 2)
-        quantise_w(grouped[0], 0, 0)
+        quantise_w(grouped[0][:], 0, 0)
         gather_x(0, 1)
-        quantise_w(grouped[1], 0, 2)
+        quantise_w(grouped[1][:], 0, 2)
         v_table = keep.tile([P, G], I32, name="v_table", tag="table0", align_bytes=64)
         nc.sync.dma_start(out=v_table[:], in_=words(v_words[0]))
 
@@ -144,9 +144,12 @@ def tile_picked_zcbow_relu_p_kernel(
         nc.scalar.copy(out=gate_sb[:].rearrange("p d v -> p (d v)"), in_=gate_ps[:].rearrange("p c t -> p (c t)"))
 
         grouped = grouped_tile("grouped_low", 2, "grouped_low")
-        group_w(nc.scalar.copy, grouped[:], w_low[:], 0, 2)
-        quantise_w(grouped, 1, 0)
+        group_w(nc.vector.tensor_copy, grouped[:], w_low[:], 0, 2)
+        quantise_w(grouped[:], 1, 0)
         gather_x(1, PARTS)
+        grouped = grouped_tile("grouped_high", 2, "grouped_high")
+        group_w(nc.vector.tensor_copy, grouped[:], w_high[:], 0, 2)
+        quantise_w(grouped[:], 1, 2)
 
         def first_product(tile_no, parts, banks):
             sums = []
@@ -187,12 +190,7 @@ def tile_picked_zcbow_relu_p_kernel(
                 nc.tensor.matmul(z_ps, lhsT=terms[d], rhs=ident[:], is_transpose=True, start=(d == 0), stop=(d == 1))
 
         h_sb = [relu_out(0, first_product(0, PARTS, ["bank_z0", "bank_z1"]), "h_sb0")]
-        sums = first_product(1, 1, ["bank_last0"])
-        for u, engine_copy, tag in ((0, nc.vector.tensor_copy, "grouped2"), (1, nc.scalar.copy, "w_codes10")):
-            grouped = grouped_tile("grouped_high%d" % u, 1, tag)
-            group_w(engine_copy, grouped[:], w_high[:], u, 1)
-            quantise_w(grouped, 1, 2 + u)
-        h_sb.append(relu_out(1, sums, "w_high"))
+        h_sb.append(relu_out(1, first_product(1, 1, ["bank_last0"]), "h_sb1"))
         h_sb.append(relu_out(2, first_product(2, 1, ["bank_last1"]), "h_sb2"))
         h_sb.append(relu_out(3, first_product(3, 1, ["bank_y0"]), "h_sb3"))
 
@@ -210,9 +208,9 @@ def tile_picked_zcbow_relu_p_kernel(
             pairs = z_rows[w][:, u].rearrange("t half c -> t (half c)").bitcast(F32)
             nc.tensor.transpose(back_ps[w][:, u, :], pairs, ident[:])
 
-        terms = []
-        for tile_no, tag in enumerate(("terms0", "terms1", "terms2")):
-            terms.append(keep.tile([P, 2, V], F32, name="terms%d" % tile_no, tag=tag, align_bytes=64))
+        early_terms = keep.tile([P, ROW_TILES - 1, 2, V], F32, name="early_terms", tag="w_high", align_bytes=64)
+        terms = [early_terms[:, tile_no] for tile_no in range(ROW_TILES - 1)]
+        for tile_no in range(ROW_TILES - 1):
             for d in range(2):
                 gather_term(terms[tile_no][:, d, :], h_sb[tile_no], d, 0, 1)
         z_ps = [psum.tile([P, 3, P], F32, name="z_ps%d" % w, tag="bank_z%d" % w) for w in range(WINDOW_TILES)]

@@ -25,7 +25,9 @@ WINDOW_TILES = V // P
 ROW_TILES = H // P
 PARTS = 2
 HALF = H // 2
-HEAD = T // 4
+HEAD = T // 2
+QUADS = HALF // 4
+SCALAR_QUADS = 24
 FLOPS = 2 * K * H * S + 2 * H * V * R
 
 
@@ -41,7 +43,7 @@ def tile_picked_zcbow_relu_p_kernel(
         pos_sb = [keep.tile([P, V // LIST], U16, name="pos_sb%d" % d) for d in range(2)]
         cand_sb = keep.tile([P, R // LIST], U16, name="cand_sb")
         x_table = [keep.tile([P, T], I32, name="x_table%d" % g, tag="table%d" % g, align_bytes=64) for g in range(PASSES)]
-        xs_table = keep.tile([P, PASSES, T], U8, name="xs_table", align_bytes=64)
+        xs_table = keep.tile([P, T], U8, name="xs_table", align_bytes=64)
         vs_table = keep.tile([P, G], U8, name="vs_table")
         x_scale = keep.tile([P, PASSES, S], U8, name="x_scale", align_bytes=64)
         ident = keep.tile([P, P], F32, name="ident")
@@ -64,10 +66,10 @@ def tile_picked_zcbow_relu_p_kernel(
         def w_rows(g):
             return w1[g * P * PACK : (g + 1) * P * PACK, :].rearrange("(p j) c -> p j c", j=PACK)
 
-        def group_w(engine_copy, grouped, columns, first, count):
+        def group_w(engine_copy, grouped, columns, quads):
             engine_copy(
-                out=grouped.rearrange("p (u m e j) -> p m j u e", u=count, e=2, j=PACK),
-                in_=columns.rearrange("p j (m u e) -> p m j u e", u=2, e=2)[:, :, :, first : first + count, :],
+                out=grouped.rearrange("p (u m e j) -> p m j u e", u=2, e=2, j=PACK)[:, quads],
+                in_=columns.rearrange("p j (m u e) -> p m j u e", u=2, e=2)[:, quads],
             )
 
         def grouped_tile(name, row_tiles, tag):
@@ -91,22 +93,22 @@ def tile_picked_zcbow_relu_p_kernel(
         w_high = keep.tile([P, PACK, HALF], F32, name="w_high", tag="w_high", align_bytes=64)
         nc.sync.dma_start(out=x_table[0][:, 0:HEAD], in_=words(x_words[0])[:, 0:HEAD])
         nc.sync.dma_start(offs_sb[:], offs)
+        nc.sync.dma_start(out=xs_table[0 : P : SPREAD // 2].bitcast(I32), in_=x_scales.rearrange("g n c -> n g c").bitcast(I32))
         nc.sync.dma_start(cand_sb[:], cand)
-        nc.sync.dma_start(out=xs_table[0:P:SPREAD].bitcast(I32), in_=x_scales.rearrange("g n c -> n g c").bitcast(I32))
-        nc.sync.dma_start(out=w_first[:], in_=w_rows(0))
         nc.sync.dma_start(out=vs_table[SPREAD // 2 : P : SPREAD].bitcast(I32), in_=v_scales[0].bitcast(I32))
+        nc.sync.dma_start(out=w_first[:], in_=w_rows(0))
         nc.sync.dma_start(out=x_table[0][:, HEAD:T], in_=words(x_words[0])[:, HEAD:T])
         nc.sync.dma_start(out=gate_rows[0:4, :], in_=gate[:, 0, :].rearrange("d (w c) -> d w c", c=P))
-        nc.sync.dma_start(out=w_low[:], in_=w_rows(1)[:, :, 0:HALF])
-
-        xs_picked = keep.tile([P, PASSES, S], U8, name="xs_picked")
-        for g in range(PASSES):
-            nc.vector.tensor_copy(xs_picked[:, g, :], xs_table[:, g, :].indirect(offs_sb[:]))
-        for r in range(4):
-            nc.sync.dma_start(
-                out=x_scale[r:P:QUADRANT].bitcast(I32), in_=xs_picked[SPREAD * r : P : QUADRANT].bitcast(I32)
-            )
         nc.sync.dma_start(out=x_table[1][:], in_=words(x_words[1]))
+
+        xs_picked = keep.tile([P, S], U8, name="xs_picked")
+        nc.vector.tensor_copy(xs_picked[:], xs_table[:].indirect(offs_sb[:]))
+        for q in range(4):
+            nc.sync.dma_start(
+                out=x_scale[QUADRANT * q : QUADRANT * q + 4].bitcast(I32),
+                in_=xs_picked[QUADRANT * q : QUADRANT * (q + 1) : SPREAD // 2].bitcast(I32),
+            )
+        nc.sync.dma_start(out=w_low[:], in_=w_rows(1)[:, :, 0:HALF])
         nc.sync.dma_start(out=w_high[:], in_=w_rows(1)[:, :, HALF:H])
         nc.sync.dma_start(pos_sb[0][:], pos1)
         nc.sync.dma_start(pos_sb[1][:], pos2)
@@ -126,7 +128,7 @@ def tile_picked_zcbow_relu_p_kernel(
 
         grouped = [grouped_tile("grouped_first%d" % half, 2, "grouped_first%d" % half) for half in range(2)]
         for half in range(2):
-            group_w(nc.scalar.copy, grouped[half][:], w_first[:, :, half * HALF : (half + 1) * HALF], 0, 2)
+            group_w(nc.scalar.copy, grouped[half][:], w_first[:, :, half * HALF : (half + 1) * HALF], slice(0, QUADS))
         quantise_w(grouped[0][:], 0, 0)
         gather_x(0, 1)
         quantise_w(grouped[1][:], 0, 2)
@@ -143,12 +145,14 @@ def tile_picked_zcbow_relu_p_kernel(
         gate_sb = keep.tile([P, 2, V], F32, name="gate_sb")
         nc.scalar.copy(out=gate_sb[:].rearrange("p d v -> p (d v)"), in_=gate_ps[:].rearrange("p c t -> p (c t)"))
 
+        gather_x(1, 1)
         grouped = grouped_tile("grouped_low", 2, "grouped_low")
-        group_w(nc.vector.tensor_copy, grouped[:], w_low[:], 0, 2)
-        quantise_w(grouped[:], 1, 0)
-        gather_x(1, PARTS)
+        group_w(nc.scalar.copy, grouped[:], w_low[:], slice(0, SCALAR_QUADS))
+        group_w(nc.vector.tensor_copy, grouped[:], w_low[:], slice(SCALAR_QUADS, QUADS))
+        for u in range(2):
+            quantise_w(grouped[:, u * P * PACK : (u + 1) * P * PACK], 1, u)
         grouped = grouped_tile("grouped_high", 2, "grouped_high")
-        group_w(nc.vector.tensor_copy, grouped[:], w_high[:], 0, 2)
+        group_w(nc.vector.tensor_copy, grouped[:], w_high[:], slice(0, QUADS))
         quantise_w(grouped[:], 1, 2)
 
         def first_product(tile_no, parts, banks):
@@ -208,37 +212,70 @@ def tile_picked_zcbow_relu_p_kernel(
             pairs = z_rows[w][:, u].rearrange("t half c -> t (half c)").bitcast(F32)
             nc.tensor.transpose(back_ps[w][:, u, :], pairs, ident[:])
 
-        early_terms = keep.tile([P, ROW_TILES - 1, 2, V], F32, name="early_terms", tag="w_high", align_bytes=64)
-        terms = [early_terms[:, tile_no] for tile_no in range(ROW_TILES - 1)]
-        for tile_no in range(ROW_TILES - 1):
+        early_terms = keep.tile([P, 2, 2, V], F32, name="early_terms", tag="w_high", align_bytes=64)
+        for tile_no in range(2):
             for d in range(2):
-                gather_term(terms[tile_no][:, d, :], h_sb[tile_no], d, 0, 1)
-        z_ps = [psum.tile([P, 3, P], F32, name="z_ps%d" % w, tag="bank_z%d" % w) for w in range(WINDOW_TILES)]
+                gather_term(early_terms[:, tile_no, d, :], h_sb[tile_no], d, 0, 1)
+
+        plain = [keep.tile([P, 2, P], F32, name="plain%d" % w) for w in range(WINDOW_TILES)]
         for w in range(WINDOW_TILES):
-            for tile_no in range(2):
-                add_turned(z_ps[w][:, tile_no, :], [terms[tile_no][:, d, w * P : (w + 1) * P] for d in range(2)])
-            nc.scalar.copy(out=z_rows[w][:, :, 0, :], in_=z_ps[w][:, 0:2, :])
+            for d in range(2):
+                nc.scalar.activation(
+                    out=plain[w][:, d, :], in_=h_sb[2][:].indirect(list_part(pos_sb[d], w, WINDOW_TILES)), func=ACT.Copy
+                )
+        last_terms = [keep.tile([P, 2, P], F32, name="last_terms%d" % w) for w in range(WINDOW_TILES)]
         for w in range(WINDOW_TILES):
-            add_turned(z_ps[w][:, 2, :], [terms[2][:, d, w * P : (w + 1) * P] for d in range(2)])
-            nc.scalar.copy(out=z_rows[w][:, 0, 1, :], in_=z_ps[w][:, 2, :])
-            turn_back(w, 0)
+            for d in range(2):
+                gather_term(last_terms[w][:, d, :], h_sb[3], d, w, WINDOW_TILES)
+
+        z_ps = [psum.tile([P, 2, P], F32, name="z_ps%d" % w, tag="bank_z%d" % w) for w in range(WINDOW_TILES)]
+        plain_ps = [psum.tile([P, 2, P], F32, name="plain_ps%d" % w, tag="bank_y%d" % w) for w in range(WINDOW_TILES)]
+        last_ps = [psum.tile([P, P], F32, name="last_ps%d" % w, tag="bank_last%d" % w) for w in range(WINDOW_TILES)]
+
+        def turn_early(tile_no):
+            for w in range(WINDOW_TILES):
+                add_turned(z_ps[w][:, tile_no, :], [early_terms[:, tile_no, d, w * P : (w + 1) * P] for d in range(2)])
+
+        def turn_plain(w):
+            for d in range(2):
+                nc.tensor.transpose(plain_ps[w][:, d, :], plain[w][:, d, :], ident[:])
+
+        turn_early(0)
+        turn_plain(0)
+        turn_early(1)
+        turn_plain(1)
+        for w in range(WINDOW_TILES):
+            add_turned(last_ps[w][:], [last_terms[w][:, d, :] for d in range(2)])
+
+        first_term = keep.tile([P, WINDOW_TILES, P], F32, name="first_term", tag="v_codes", align_bytes=64)
+        for w in range(WINDOW_TILES):
+            nc.scalar.activation(
+                out=first_term[:, w, :], in_=plain_ps[w][:, 0, :], func=ACT.Copy, scale=gate_column[:, w : w + 1]
+            )
+            nc.vector.scalar_tensor_tensor(
+                out=z_rows[w][:, 0, 1, :],
+                in0=plain_ps[w][:, 1, :],
+                scalar=gate_column[:, WINDOW_TILES + w : WINDOW_TILES + w + 1],
+                in1=first_term[:, w, :],
+                op0=ALU.mult,
+                op1=ALU.add,
+            )
+            nc.scalar.copy(out=z_rows[w][:, :, 0, :], in_=z_ps[w][:])
+        for w in range(WINDOW_TILES):
+            nc.scalar.copy(out=z_rows[w][:, 1, 1, :], in_=last_ps[w][:])
+        for w in range(WINDOW_TILES):
+            for u in range(2):
+                turn_back(w, u)
 
         z_grouped = []
         for w in range(WINDOW_TILES):
-            last_terms = keep.tile([P, 2, P], F32, name="last_terms%d" % w)
-            for d in range(2):
-                gather_term(last_terms[:, d, :], h_sb[3], d, w, WINDOW_TILES)
-            last_ps = psum.tile([P, P], F32, name="last_ps%d" % w, tag="bank_last%d" % w)
-            add_turned(last_ps[:], [last_terms[:, d, :] for d in range(2)])
-            nc.scalar.copy(out=z_rows[w][:, 1, 1, :], in_=last_ps[:])
-            turn_back(w, 1)
             z_grouped.append(keep.tile([P, P * PACK], BF16, name="z_grouped%d" % w, align_bytes=64))
             nc.scalar.copy(
                 out=z_grouped[w][:].bitcast(F32).rearrange("p (t u) -> p t u", u=2),
                 in_=back_ps[w][:].rearrange("p u t -> p t u"),
             )
 
-        v_codes = keep.tile([P, R], U32, name="v_codes", tag="h_sb3", align_bytes=64)
+        v_codes = keep.tile([P, R], U32, name="v_codes", tag="v_codes", align_bytes=64)
         nc.vector.tensor_copy(v_codes[:], v_table[:].bitcast(U32).indirect(cand_sb[:]))
 
         y_ps = []
@@ -246,7 +283,7 @@ def tile_picked_zcbow_relu_p_kernel(
             z_codes = keep.tile([P, P], U32, name="z_codes%d" % w, align_bytes=64)
             z_scale = keep.tile([P, P], U8, name="z_scale%d" % w, align_bytes=64)
             nc.vector.quantize_mx(out=z_codes[:].bitcast(FP8X4), scales=z_scale[:], in_=z_grouped[w][:])
-            y_ps.append(psum.tile([P, R], F32, name="y_ps%d" % w, tag="bank_y%d" % w))
+            y_ps.append(psum.tile([P, R], F32, name="y_ps%d" % w, tag="bank_z%d" % w))
             nc.tensor.matmul_mx(
                 out=y_ps[w][:],
                 lhsT=z_codes[:].bitcast(FP8X4),

@@ -37,6 +37,7 @@ def tile_picked_zcbow_relu_p_kernel(
     nc = tc.nc
     with ExitStack() as ctx:
         keep = ctx.enter_context(tc.tile_pool(name="keep", bufs=1))
+        reused = ctx.enter_context(tc.tile_pool(name="reused", bufs=1))
         psum = ctx.enter_context(tc.psum_pool(name="psum", bufs=1))
 
         offs_sb = keep.tile([P, S // LIST], U16, name="offs_sb")
@@ -135,11 +136,13 @@ def tile_picked_zcbow_relu_p_kernel(
         v_table = keep.tile([P, G], I32, name="v_table", tag="table0", align_bytes=64)
         nc.sync.dma_start(out=v_table[:], in_=words(v_words[0]))
 
-        column_ps = psum.tile([P, P], F32, name="column_ps", tag="bank_back0")
+        column_ps = psum.tile([P, P], F32, name="column_ps", tag="bank5")
         nc.tensor.transpose(column_ps[:], gate_rows[:], ident[:])
         gate_column = keep.tile([P, 4], F32, name="gate_column")
         nc.scalar.copy(out=gate_column[:], in_=column_ps[:, 0:4])
-        gate_ps = psum.tile([P, 4, P], F32, name="gate_ps", tag="bank_back1")
+        first_gate = reused.tile([P, 1], F32, name="first_gate", offset=2 * P * 4, align_bytes=64)
+        nc.scalar.copy(out=first_gate[:], in_=column_ps[:, 0:1])
+        gate_ps = psum.tile([P, 4, P], F32, name="gate_ps", tag="bank6")
         for c in range(4):
             nc.tensor.transpose(gate_ps[:, c, :], gate_column[:, c : c + 1].to_broadcast([P, P]), ident[:])
         gate_sb = keep.tile([P, 2, V], F32, name="gate_sb")
@@ -189,14 +192,10 @@ def tile_picked_zcbow_relu_p_kernel(
                 ALU.mult,
             )
 
-        def add_turned(z_ps, terms):
-            for d in range(2):
-                nc.tensor.matmul(z_ps, lhsT=terms[d], rhs=ident[:], is_transpose=True, start=(d == 0), stop=(d == 1))
-
-        h_sb = [relu_out(0, first_product(0, PARTS, ["bank_z0", "bank_z1"]), "h_sb0")]
-        h_sb.append(relu_out(1, first_product(1, 1, ["bank_last0"]), "h_sb1"))
-        h_sb.append(relu_out(2, first_product(2, 1, ["bank_last1"]), "h_sb2"))
-        h_sb.append(relu_out(3, first_product(3, 1, ["bank_y0"]), "h_sb3"))
+        h_sb = [relu_out(0, first_product(0, PARTS, ["bank0", "bank1"]), "h_sb0")]
+        h_sb.append(relu_out(1, first_product(1, 1, ["bank2"]), "h_sb1"))
+        h_sb.append(relu_out(2, first_product(2, 1, ["bank3"]), "h_sb2"))
+        h_sb.append(relu_out(3, first_product(3, 1, ["bank4"]), "h_sb3"))
 
         v_scale = x_scale[4:P, 0, :]
         for r in range(4):
@@ -205,8 +204,11 @@ def tile_picked_zcbow_relu_p_kernel(
                 in_=vs_picked[SPREAD * r + SPREAD // 2 : P : QUADRANT].bitcast(I32),
             )
 
-        z_rows = [keep.tile([P, 2, 2, P], BF16, name="z_rows%d" % w) for w in range(WINDOW_TILES)]
-        back_ps = [psum.tile([P, 2, P], F32, name="back_ps%d" % w, tag="bank_back%d" % w) for w in range(WINDOW_TILES)]
+        z_rows = [
+            reused.tile([P, 2, 2, P], BF16, name="z_rows%d" % w, offset=2048 + 1024 * w, align_bytes=64)
+            for w in range(WINDOW_TILES)
+        ]
+        back_ps = [psum.tile([P, 2, P], F32, name="back_ps%d" % w, tag="bank%d" % (3 - 2 * w)) for w in range(WINDOW_TILES)]
 
         def turn_back(w, u):
             pairs = z_rows[w][:, u].rearrange("t half c -> t (half c)").bitcast(F32)
@@ -217,52 +219,60 @@ def tile_picked_zcbow_relu_p_kernel(
             for d in range(2):
                 gather_term(early_terms[:, tile_no, d, :], h_sb[tile_no], d, 0, 1)
 
-        plain = [keep.tile([P, 2, P], F32, name="plain%d" % w) for w in range(WINDOW_TILES)]
-        for w in range(WINDOW_TILES):
+        late_terms = [keep.tile([P, 2, P], F32, name="late_terms%d" % u) for u in range(2)]
+        for u in range(2):
             for d in range(2):
+                gather_term(late_terms[u][:, d, :], h_sb[2 + u], d, 1, WINDOW_TILES)
+        plain = [
+            reused.tile([P, 2, P], F32, name="plain%d" % d, offset=(2048 + 512) * (1 - d), align_bytes=64) for d in range(2)
+        ]
+        for d in range(2):
+            for u in range(2):
                 nc.scalar.activation(
-                    out=plain[w][:, d, :], in_=h_sb[2][:].indirect(list_part(pos_sb[d], w, WINDOW_TILES)), func=ACT.Copy
+                    out=plain[d][:, u, :], in_=h_sb[2 + u][:].indirect(list_part(pos_sb[d], 0, WINDOW_TILES)), func=ACT.Copy
                 )
-        last_terms = [keep.tile([P, 2, P], F32, name="last_terms%d" % w) for w in range(WINDOW_TILES)]
-        for w in range(WINDOW_TILES):
-            for d in range(2):
-                gather_term(last_terms[w][:, d, :], h_sb[3], d, w, WINDOW_TILES)
 
-        z_ps = [psum.tile([P, 2, P], F32, name="z_ps%d" % w, tag="bank_z%d" % w) for w in range(WINDOW_TILES)]
-        plain_ps = [psum.tile([P, 2, P], F32, name="plain_ps%d" % w, tag="bank_y%d" % w) for w in range(WINDOW_TILES)]
-        last_ps = [psum.tile([P, P], F32, name="last_ps%d" % w, tag="bank_last%d" % w) for w in range(WINDOW_TILES)]
+        early_ps = psum.tile([P, 2, P], F32, name="early_ps", tag="bank5")
+        sums_ps = psum.tile([P, 3, P], F32, name="sums_ps", tag="bank6")
+        plain_ps = [psum.tile([P, 2, P], F32, name="plain_ps%d" % d, tag="bank%d" % d) for d in range(2)]
+        last_ps = psum.tile([P, P], F32, name="last_ps", tag="bank2")
 
-        def turn_early(tile_no):
-            for w in range(WINDOW_TILES):
-                add_turned(z_ps[w][:, tile_no, :], [early_terms[:, tile_no, d, w * P : (w + 1) * P] for d in range(2)])
+        def turn_term(target, term, d):
+            nc.tensor.matmul(target, lhsT=term, rhs=ident[:], is_transpose=True, start=(d == 0), stop=(d == 1))
 
-        def turn_plain(w):
-            for d in range(2):
-                nc.tensor.transpose(plain_ps[w][:, d, :], plain[w][:, d, :], ident[:])
+        def turn_early(tile_no, d):
+            turn_term(early_ps[:, tile_no, :], early_terms[:, tile_no, d, 0:P], d)
+            turn_term(sums_ps[:, tile_no, :], early_terms[:, tile_no, d, P : 2 * P], d)
 
-        turn_early(0)
+        def turn_plain(d):
+            for u in range(2):
+                nc.tensor.transpose(plain_ps[d][:, u, :], plain[d][:, u, :], ident[:])
+
+        turn_early(0, 0)
+        turn_early(0, 1)
+        turn_early(1, 0)
         turn_plain(0)
-        turn_early(1)
+        turn_early(1, 1)
+        turn_term(sums_ps[:, 2, :], late_terms[0][:, 0, :], 0)
         turn_plain(1)
-        for w in range(WINDOW_TILES):
-            add_turned(last_ps[w][:], [last_terms[w][:, d, :] for d in range(2)])
+        turn_term(sums_ps[:, 2, :], late_terms[0][:, 1, :], 1)
+        for d in range(2):
+            turn_term(last_ps[:], late_terms[1][:, d, :], d)
 
-        first_term = keep.tile([P, WINDOW_TILES, P], F32, name="first_term", tag="v_codes", align_bytes=64)
-        for w in range(WINDOW_TILES):
-            nc.scalar.activation(
-                out=first_term[:, w, :], in_=plain_ps[w][:, 0, :], func=ACT.Copy, scale=gate_column[:, w : w + 1]
-            )
-            nc.vector.scalar_tensor_tensor(
-                out=z_rows[w][:, 0, 1, :],
-                in0=plain_ps[w][:, 1, :],
-                scalar=gate_column[:, WINDOW_TILES + w : WINDOW_TILES + w + 1],
-                in1=first_term[:, w, :],
-                op0=ALU.mult,
-                op1=ALU.add,
-            )
-            nc.scalar.copy(out=z_rows[w][:, :, 0, :], in_=z_ps[w][:])
-        for w in range(WINDOW_TILES):
-            nc.scalar.copy(out=z_rows[w][:, 1, 1, :], in_=last_ps[w][:])
+        first_term = keep.tile([P, 2, P], F32, name="first_term")
+        nc.scalar.activation(out=first_term[:], in_=plain_ps[0][:], func=ACT.Copy, scale=first_gate[:])
+        nc.vector.scalar_tensor_tensor(
+            out=z_rows[0][:, :, 1, :],
+            in0=plain_ps[1][:],
+            scalar=gate_column[:, WINDOW_TILES : WINDOW_TILES + 1],
+            in1=first_term[:],
+            op0=ALU.mult,
+            op1=ALU.add,
+        )
+        nc.scalar.copy(out=z_rows[0][:, :, 0, :], in_=early_ps[:])
+        nc.scalar.copy(out=z_rows[1][:, :, 0, :], in_=sums_ps[:, 0:2, :])
+        nc.scalar.copy(out=z_rows[1][:, 0, 1, :], in_=sums_ps[:, 2, :])
+        nc.scalar.copy(out=z_rows[1][:, 1, 1, :], in_=last_ps[:])
         for w in range(WINDOW_TILES):
             for u in range(2):
                 turn_back(w, u)
@@ -275,7 +285,7 @@ def tile_picked_zcbow_relu_p_kernel(
                 in_=back_ps[w][:].rearrange("p u t -> p t u"),
             )
 
-        v_codes = keep.tile([P, R], U32, name="v_codes", tag="v_codes", align_bytes=64)
+        v_codes = reused.tile([P, R], U32, name="v_codes", offset=0, align_bytes=64)
         nc.vector.tensor_copy(v_codes[:], v_table[:].bitcast(U32).indirect(cand_sb[:]))
 
         y_ps = []
@@ -283,7 +293,7 @@ def tile_picked_zcbow_relu_p_kernel(
             z_codes = keep.tile([P, P], U32, name="z_codes%d" % w, align_bytes=64)
             z_scale = keep.tile([P, P], U8, name="z_scale%d" % w, align_bytes=64)
             nc.vector.quantize_mx(out=z_codes[:].bitcast(FP8X4), scales=z_scale[:], in_=z_grouped[w][:])
-            y_ps.append(psum.tile([P, R], F32, name="y_ps%d" % w, tag="bank_z%d" % w))
+            y_ps.append(psum.tile([P, R], F32, name="y_ps%d" % w, tag="bank%d" % (7 - 2 * w)))
             nc.tensor.matmul_mx(
                 out=y_ps[w][:],
                 lhsT=z_codes[:].bitcast(FP8X4),

@@ -140,23 +140,24 @@ def tile_picked_zcbow_relu_p_kernel(
         nc.tensor.transpose(column_ps[:], gate_rows[:], ident[:])
         gate_column = keep.tile([P, 4], F32, name="gate_column")
         nc.scalar.copy(out=gate_column[:], in_=column_ps[:, 0:4])
-        first_gate = reused.tile([P, 1], F32, name="first_gate", offset=2 * P * 4, align_bytes=64)
-        nc.scalar.copy(out=first_gate[:], in_=column_ps[:, 0:1])
+        first_gate = reused.tile([P, 1], F32, name="first_gate", offset=1536, align_bytes=64)
+        nc.scalar.copy(out=first_gate[:], in_=column_ps[:, 1:2])
         gate_ps = psum.tile([P, 4, P], F32, name="gate_ps", tag="bank6")
         for c in range(4):
             nc.tensor.transpose(gate_ps[:, c, :], gate_column[:, c : c + 1].to_broadcast([P, P]), ident[:])
-        gate_sb = keep.tile([P, 2, V], F32, name="gate_sb")
-        nc.scalar.copy(out=gate_sb[:].rearrange("p d v -> p (d v)"), in_=gate_ps[:].rearrange("p c t -> p (c t)"))
+        gate_sb = [
+            reused.tile([P, V], F32, name="gate_sb0", offset=6656, align_bytes=64),
+            keep.tile([P, V], F32, name="gate_sb1"),
+        ]
+        for d in range(2):
+            nc.scalar.copy(out=gate_sb[d][:], in_=gate_ps[:, 2 * d : 2 * d + 2, :].rearrange("p c t -> p (c t)"))
 
         gather_x(1, 1)
         grouped = grouped_tile("grouped_low", 2, "grouped_low")
         group_w(nc.scalar.copy, grouped[:], w_low[:], slice(0, SCALAR_QUADS))
         group_w(nc.vector.tensor_copy, grouped[:], w_low[:], slice(SCALAR_QUADS, QUADS))
-        for u in range(2):
+        for u in (1, 0):
             quantise_w(grouped[:, u * P * PACK : (u + 1) * P * PACK], 1, u)
-        grouped = grouped_tile("grouped_high", 2, "grouped_high")
-        group_w(nc.vector.tensor_copy, grouped[:], w_high[:], slice(0, QUADS))
-        quantise_w(grouped[:], 1, 2)
 
         def first_product(tile_no, parts, banks):
             sums = []
@@ -176,26 +177,51 @@ def tile_picked_zcbow_relu_p_kernel(
                 sums.append(h_ps)
             return sums
 
-        def relu_out(tile_no, sums, tag):
-            h_tile = keep.tile([P, S], F32, name="h_sb%d" % tile_no, tag=tag, align_bytes=64)
-            for part, h_ps in enumerate(sums):
-                entries = slice(part * S // len(sums), (part + 1) * S // len(sums))
-                nc.scalar.activation(out=h_tile[:, entries], in_=h_ps[:], func=ACT.Relu)
-            return h_tile
-
         def gather_term(term, h_tile, d, part, parts):
             count = V // parts
             nc.vector.tensor_tensor(
                 term,
                 h_tile[:].indirect(list_part(pos_sb[d], part, parts)),
-                gate_sb[:, d, part * count : (part + 1) * count],
+                gate_sb[d][:, part * count : (part + 1) * count],
                 ALU.mult,
             )
 
-        h_sb = [relu_out(0, first_product(0, PARTS, ["bank0", "bank1"]), "h_sb0")]
-        h_sb.append(relu_out(1, first_product(1, 1, ["bank2"]), "h_sb1"))
-        h_sb.append(relu_out(2, first_product(2, 1, ["bank3"]), "h_sb2"))
-        h_sb.append(relu_out(3, first_product(3, 1, ["bank4"]), "h_sb3"))
+        h_sb = {}
+        for tile_no in range(ROW_TILES):
+            h_sb[tile_no] = keep.tile([P, S], F32, name="h_sb%d" % tile_no, align_bytes=64)
+
+        def relu_whole(tile_no, bank):
+            nc.scalar.activation(out=h_sb[tile_no][:], in_=first_product(tile_no, 1, [bank])[0][:], func=ACT.Relu)
+
+        halves = first_product(1, PARTS, ["bank0", "bank1"])
+        grouped = grouped_tile("grouped_high", 2, "grouped_high")
+        group_w(nc.vector.tensor_copy, grouped[:], w_high[:], slice(0, QUADS))
+        nc.scalar.activation(out=h_sb[1][:, 0 : S // 2], in_=halves[0][:], func=ACT.Relu)
+        nc.vector.tensor_scalar(out=h_sb[1][:, S // 2 : S], in0=halves[1][:], scalar1=0.0, scalar2=None, op0=ALU.max)
+        quantise_w(grouped[:], 1, 2)
+        relu_whole(0, "bank2")
+
+        plain = [
+            reused.tile([P, 3, P], F32, name="plain%d" % d, offset=(2048 + 256) * (1 - d), align_bytes=64) for d in range(2)
+        ]
+
+        def slot(tile_no):
+            return 2 * (tile_no % 2) + tile_no // 2
+
+        def gather_plain(tile_no, d):
+            nc.scalar.activation(
+                out=plain[d][:, slot(tile_no) - 1, :],
+                in_=h_sb[tile_no][:].indirect(list_part(pos_sb[d], 1, WINDOW_TILES)),
+                func=ACT.Copy,
+            )
+
+        for d in range(2):
+            gather_plain(1, d)
+        relu_whole(2, "bank3")
+        relu_whole(3, "bank4")
+        for d in range(2):
+            for tile_no in (2, 3):
+                gather_plain(tile_no, d)
 
         v_scale = x_scale[4:P, 0, :]
         for r in range(4):
@@ -204,78 +230,75 @@ def tile_picked_zcbow_relu_p_kernel(
                 in_=vs_picked[SPREAD * r + SPREAD // 2 : P : QUADRANT].bitcast(I32),
             )
 
-        z_rows = [
-            reused.tile([P, 2, 2, P], BF16, name="z_rows%d" % w, offset=2048 + 1024 * w, align_bytes=64)
-            for w in range(WINDOW_TILES)
-        ]
-        back_ps = [psum.tile([P, 2, P], F32, name="back_ps%d" % w, tag="bank%d" % (3 - 2 * w)) for w in range(WINDOW_TILES)]
-
-        def turn_back(w, u):
-            pairs = z_rows[w][:, u].rearrange("t half c -> t (half c)").bitcast(F32)
-            nc.tensor.transpose(back_ps[w][:, u, :], pairs, ident[:])
-
-        early_terms = keep.tile([P, 2, 2, V], F32, name="early_terms", tag="w_high", align_bytes=64)
-        for tile_no in range(2):
-            for d in range(2):
-                gather_term(early_terms[:, tile_no, d, :], h_sb[tile_no], d, 0, 1)
-
-        late_terms = [keep.tile([P, 2, P], F32, name="late_terms%d" % u) for u in range(2)]
-        for u in range(2):
-            for d in range(2):
-                gather_term(late_terms[u][:, d, :], h_sb[2 + u], d, 1, WINDOW_TILES)
-        plain = [
-            reused.tile([P, 2, P], F32, name="plain%d" % d, offset=(2048 + 512) * (1 - d), align_bytes=64) for d in range(2)
-        ]
+        terms = keep.tile([P, 2, ROW_TILES + 1, P], F32, name="terms", tag="w_high", align_bytes=64)
         for d in range(2):
-            for u in range(2):
-                nc.scalar.activation(
-                    out=plain[d][:, u, :], in_=h_sb[2 + u][:].indirect(list_part(pos_sb[d], 0, WINDOW_TILES)), func=ACT.Copy
-                )
+            gather_term(terms[:, d, 2, :], h_sb[1], d, 0, WINDOW_TILES)
+        for d in range(2):
+            gather_term(terms[:, d, 0:2, :].rearrange("p w c -> p (w c)"), h_sb[0], d, 0, 1)
+        for tile_no in (2, 3):
+            for d in range(2):
+                gather_term(terms[:, d, tile_no + 1, :], h_sb[tile_no], d, 0, WINDOW_TILES)
 
-        early_ps = psum.tile([P, 2, P], F32, name="early_ps", tag="bank5")
-        sums_ps = psum.tile([P, 3, P], F32, name="sums_ps", tag="bank6")
-        plain_ps = [psum.tile([P, 2, P], F32, name="plain_ps%d" % d, tag="bank%d" % d) for d in range(2)]
+        plain_ps = [psum.tile([P, 3, P], F32, name="plain_ps%d" % d, tag="bank%d" % d) for d in range(2)]
+        sums_ps = psum.tile([P, 3, P], F32, name="sums_ps", tag="bank5")
+        other_ps = psum.tile([P, P], F32, name="other_ps", tag="bank6")
         last_ps = psum.tile([P, P], F32, name="last_ps", tag="bank2")
 
-        def turn_term(target, term, d):
-            nc.tensor.matmul(target, lhsT=term, rhs=ident[:], is_transpose=True, start=(d == 0), stop=(d == 1))
+        def turn_term(target, place, d):
+            nc.tensor.matmul(
+                target, lhsT=terms[:, d, place, :], rhs=ident[:], is_transpose=True, start=(d == 0), stop=(d == 1)
+            )
 
-        def turn_early(tile_no, d):
-            turn_term(early_ps[:, tile_no, :], early_terms[:, tile_no, d, 0:P], d)
-            turn_term(sums_ps[:, tile_no, :], early_terms[:, tile_no, d, P : 2 * P], d)
+        def turn_plain(tile_no, d):
+            place = slot(tile_no) - 1
+            nc.tensor.transpose(plain_ps[d][:, place, :], plain[d][:, place, :], ident[:])
 
-        def turn_plain(d):
-            for u in range(2):
-                nc.tensor.transpose(plain_ps[d][:, u, :], plain[d][:, u, :], ident[:])
-
-        turn_early(0, 0)
-        turn_early(0, 1)
-        turn_early(1, 0)
-        turn_plain(0)
-        turn_early(1, 1)
-        turn_term(sums_ps[:, 2, :], late_terms[0][:, 0, :], 0)
-        turn_plain(1)
-        turn_term(sums_ps[:, 2, :], late_terms[0][:, 1, :], 1)
         for d in range(2):
-            turn_term(last_ps[:], late_terms[1][:, d, :], d)
+            turn_term(sums_ps[:, slot(1), :], 2, d)
+            turn_plain(1, d)
+        for d in range(2):
+            turn_term(sums_ps[:, slot(0), :], 0, d)
+            turn_term(other_ps[:], 1, d)
+        for d in range(2):
+            turn_term(sums_ps[:, slot(2), :], 3, d)
+            turn_plain(2 + d, 0)
+        for d in range(2):
+            turn_plain(2 + d, 1)
+            turn_term(last_ps[:], 4, d)
 
-        first_term = keep.tile([P, 2, P], F32, name="first_term")
+        z_rows = [
+            reused.tile([P, ROW_TILES, P], BF16, name="z_rows%d" % w, offset=(6144, 3072)[w], align_bytes=64)
+            for w in range(WINDOW_TILES)
+        ]
+        v_codes = [
+            reused.tile([P, R // 2], U32, name="v_codes%d" % part, offset=(7168, 1024)[part], align_bytes=64)
+            for part in range(2)
+        ]
+
+        def gather_v(part):
+            nc.vector.tensor_copy(v_codes[part][:], v_table[:].bitcast(U32).indirect(list_part(cand_sb, part, 2)))
+
+        nc.vector.tensor_copy(z_rows[0][:, 0:3, :], sums_ps[:])
+        gather_v(0)
+        first_term = keep.tile([P, 3, P], F32, name="first_term")
         nc.scalar.activation(out=first_term[:], in_=plain_ps[0][:], func=ACT.Copy, scale=first_gate[:])
         nc.vector.scalar_tensor_tensor(
-            out=z_rows[0][:, :, 1, :],
+            out=z_rows[1][:, 1:ROW_TILES, :],
             in0=plain_ps[1][:],
-            scalar=gate_column[:, WINDOW_TILES : WINDOW_TILES + 1],
+            scalar=gate_column[:, 3:4],
             in1=first_term[:],
             op0=ALU.mult,
             op1=ALU.add,
         )
-        nc.scalar.copy(out=z_rows[0][:, :, 0, :], in_=early_ps[:])
-        nc.scalar.copy(out=z_rows[1][:, :, 0, :], in_=sums_ps[:, 0:2, :])
-        nc.scalar.copy(out=z_rows[1][:, 0, 1, :], in_=sums_ps[:, 2, :])
-        nc.scalar.copy(out=z_rows[1][:, 1, 1, :], in_=last_ps[:])
+        gather_v(1)
+        nc.scalar.copy(out=z_rows[0][:, 3, :], in_=last_ps[:])
+        nc.scalar.copy(out=z_rows[1][:, 0, :], in_=other_ps[:])
+
+        back_ps = [psum.tile([P, 2, P], F32, name="back_ps%d" % w, tag="bank%d" % (3 - w)) for w in range(WINDOW_TILES)]
         for w in range(WINDOW_TILES):
             for u in range(2):
-                turn_back(w, u)
+                pairs = z_rows[w][:, 2 * u : 2 * u + 2, :].rearrange("t r c -> t (r c)").bitcast(F32)
+                nc.tensor.transpose(back_ps[w][:, u, :], pairs, ident[:])
 
         z_grouped = []
         for w in range(WINDOW_TILES):
@@ -285,24 +308,23 @@ def tile_picked_zcbow_relu_p_kernel(
                 in_=back_ps[w][:].rearrange("p u t -> p t u"),
             )
 
-        v_codes = reused.tile([P, R], U32, name="v_codes", offset=0, align_bytes=64)
-        nc.vector.tensor_copy(v_codes[:], v_table[:].bitcast(U32).indirect(cand_sb[:]))
-
         y_ps = []
         for w in range(WINDOW_TILES):
             z_codes = keep.tile([P, P], U32, name="z_codes%d" % w, align_bytes=64)
             z_scale = keep.tile([P, P], U8, name="z_scale%d" % w, align_bytes=64)
             nc.vector.quantize_mx(out=z_codes[:].bitcast(FP8X4), scales=z_scale[:], in_=z_grouped[w][:])
-            y_ps.append(psum.tile([P, R], F32, name="y_ps%d" % w, tag="bank%d" % (7 - 2 * w)))
-            nc.tensor.matmul_mx(
-                out=y_ps[w][:],
-                lhsT=z_codes[:].bitcast(FP8X4),
-                lhsT_scale=z_scale[:],
-                rhs=v_codes[:].bitcast(FP8X4),
-                rhs_scale=v_scale,
-                start=True,
-                stop=True,
-            )
+            y_ps.append(psum.tile([P, R], F32, name="y_ps%d" % w, tag="bank%d" % (7 - 3 * w)))
+            for part in range(2):
+                picked = slice(part * R // 2, (part + 1) * R // 2)
+                nc.tensor.matmul_mx(
+                    out=y_ps[w][:, picked],
+                    lhsT=z_codes[:].bitcast(FP8X4),
+                    lhsT_scale=z_scale[:],
+                    rhs=v_codes[part][:].bitcast(FP8X4),
+                    rhs_scale=v_scale[:, picked],
+                    start=True,
+                    stop=True,
+                )
 
         for w in range(WINDOW_TILES):
             neg_max = keep.tile([P, 1], F32, name="neg_max%d" % w)

@@ -202,7 +202,7 @@ def tile_picked_zcbow_relu_p_kernel(
         relu_whole(0, "bank2")
 
         plain = [
-            reused.tile([P, 3, P], F32, name="plain%d" % d, offset=(2048 + 256) * (1 - d), align_bytes=64) for d in range(2)
+            reused.tile([P, 2, P], F32, name="plain%d" % d, offset=(3072, 512)[d], align_bytes=64) for d in range(2)
         ]
 
         def slot(tile_no):
@@ -220,8 +220,7 @@ def tile_picked_zcbow_relu_p_kernel(
         relu_whole(2, "bank3")
         relu_whole(3, "bank4")
         for d in range(2):
-            for tile_no in (2, 3):
-                gather_plain(tile_no, d)
+            gather_plain(2, d)
 
         v_scale = x_scale[4:P, 0, :]
         for r in range(4):
@@ -230,7 +229,7 @@ def tile_picked_zcbow_relu_p_kernel(
                 in_=vs_picked[SPREAD * r + SPREAD // 2 : P : QUADRANT].bitcast(I32),
             )
 
-        terms = keep.tile([P, 2, ROW_TILES + 1, P], F32, name="terms", tag="w_high", align_bytes=64)
+        terms = keep.tile([P, 2, ROW_TILES + 2, P], F32, name="terms", tag="w_high", align_bytes=64)
         for d in range(2):
             gather_term(terms[:, d, 2, :], h_sb[1], d, 0, WINDOW_TILES)
         for d in range(2):
@@ -238,11 +237,13 @@ def tile_picked_zcbow_relu_p_kernel(
         for tile_no in (2, 3):
             for d in range(2):
                 gather_term(terms[:, d, tile_no + 1, :], h_sb[tile_no], d, 0, WINDOW_TILES)
+        for d in range(2):
+            gather_term(terms[:, d, 5, :], h_sb[3], d, 1, WINDOW_TILES)
 
-        plain_ps = [psum.tile([P, 3, P], F32, name="plain_ps%d" % d, tag="bank%d" % d) for d in range(2)]
+        plain_ps = [psum.tile([P, 2, P], F32, name="plain_ps%d" % d, tag="bank%d" % (3 + d)) for d in range(2)]
         sums_ps = psum.tile([P, 3, P], F32, name="sums_ps", tag="bank5")
         other_ps = psum.tile([P, P], F32, name="other_ps", tag="bank6")
-        last_ps = psum.tile([P, P], F32, name="last_ps", tag="bank2")
+        last_ps = [psum.tile([P, P], F32, name="last_ps%d" % w, tag="bank%d" % w) for w in range(WINDOW_TILES)]
 
         def turn_term(target, place, d):
             nc.tensor.matmul(
@@ -255,20 +256,21 @@ def tile_picked_zcbow_relu_p_kernel(
 
         for d in range(2):
             turn_term(sums_ps[:, slot(1), :], 2, d)
-            turn_plain(1, d)
         for d in range(2):
             turn_term(sums_ps[:, slot(0), :], 0, d)
             turn_term(other_ps[:], 1, d)
         for d in range(2):
+            turn_plain(1, d)
             turn_term(sums_ps[:, slot(2), :], 3, d)
-            turn_plain(2 + d, 0)
         for d in range(2):
-            turn_plain(2 + d, 1)
-            turn_term(last_ps[:], 4, d)
+            turn_term(last_ps[0][:], 4, d)
+            turn_plain(2, d)
+        for d in range(2):
+            turn_term(last_ps[1][:], 5, d)
 
         z_rows = [
-            reused.tile([P, ROW_TILES, P], BF16, name="z_rows%d" % w, offset=(6144, 3072)[w], align_bytes=64)
-            for w in range(WINDOW_TILES)
+            keep.tile([P, ROW_TILES, P], BF16, name="z_rows0"),
+            reused.tile([P, ROW_TILES, P], BF16, name="z_rows1", offset=3072, align_bytes=64),
         ]
         v_codes = [
             reused.tile([P, R // 2], U32, name="v_codes%d" % part, offset=(7168, 1024)[part], align_bytes=64)
@@ -278,12 +280,12 @@ def tile_picked_zcbow_relu_p_kernel(
         def gather_v(part):
             nc.vector.tensor_copy(v_codes[part][:], v_table[:].bitcast(U32).indirect(list_part(cand_sb, part, 2)))
 
-        nc.vector.tensor_copy(z_rows[0][:, 0:3, :], sums_ps[:])
+        nc.scalar.copy(out=z_rows[0][:, 0:3, :], in_=sums_ps[:])
         gather_v(0)
-        first_term = keep.tile([P, 3, P], F32, name="first_term")
+        first_term = keep.tile([P, 2, P], F32, name="first_term")
         nc.scalar.activation(out=first_term[:], in_=plain_ps[0][:], func=ACT.Copy, scale=first_gate[:])
         nc.vector.scalar_tensor_tensor(
-            out=z_rows[1][:, 1:ROW_TILES, :],
+            out=z_rows[1][:, 1:3, :],
             in0=plain_ps[1][:],
             scalar=gate_column[:, 3:4],
             in1=first_term[:],
@@ -291,10 +293,11 @@ def tile_picked_zcbow_relu_p_kernel(
             op1=ALU.add,
         )
         gather_v(1)
-        nc.scalar.copy(out=z_rows[0][:, 3, :], in_=last_ps[:])
+        nc.scalar.copy(out=z_rows[0][:, 3, :], in_=last_ps[0][:])
         nc.scalar.copy(out=z_rows[1][:, 0, :], in_=other_ps[:])
+        nc.scalar.copy(out=z_rows[1][:, 3, :], in_=last_ps[1][:])
 
-        back_ps = [psum.tile([P, 2, P], F32, name="back_ps%d" % w, tag="bank%d" % (3 - w)) for w in range(WINDOW_TILES)]
+        back_ps = [psum.tile([P, 2, P], F32, name="back_ps%d" % w, tag="bank%d" % (2 - 2 * w)) for w in range(WINDOW_TILES)]
         for w in range(WINDOW_TILES):
             for u in range(2):
                 pairs = z_rows[w][:, 2 * u : 2 * u + 2, :].rearrange("t r c -> t (r c)").bitcast(F32)
@@ -313,7 +316,7 @@ def tile_picked_zcbow_relu_p_kernel(
             z_codes = keep.tile([P, P], U32, name="z_codes%d" % w, align_bytes=64)
             z_scale = keep.tile([P, P], U8, name="z_scale%d" % w, align_bytes=64)
             nc.vector.quantize_mx(out=z_codes[:].bitcast(FP8X4), scales=z_scale[:], in_=z_grouped[w][:])
-            y_ps.append(psum.tile([P, R], F32, name="y_ps%d" % w, tag="bank%d" % (7 - 3 * w)))
+            y_ps.append(psum.tile([P, R], F32, name="y_ps%d" % w, tag="bank%d" % (7 - 2 * w)))
             for part in range(2):
                 picked = slice(part * R // 2, (part + 1) * R // 2)
                 nc.tensor.matmul_mx(

@@ -90,7 +90,7 @@ def tile_picked_zcbow_relu_p_kernel(
                 w_scale[g, first_tile + n] = scale[:, n * P : (n + 1) * P]
 
         w_first = keep.tile([P, PACK, H], F32, name="w_first")
-        w_low = keep.tile([P, PACK, HALF], F32, name="w_low")
+        w_low = reused.tile([P, PACK, HALF], F32, name="w_low", offset=8192, align_bytes=64)
         w_high = keep.tile([P, PACK, HALF], F32, name="w_high", tag="w_high", align_bytes=64)
         nc.sync.dma_start(out=x_table[0][:, 0:HEAD], in_=words(x_words[0])[:, 0:HEAD])
         nc.sync.dma_start(offs_sb[:], offs)
@@ -133,8 +133,6 @@ def tile_picked_zcbow_relu_p_kernel(
         quantise_w(grouped[0][:], 0, 0)
         gather_x(0, 1)
         quantise_w(grouped[1][:], 0, 2)
-        v_table = keep.tile([P, G], I32, name="v_table", tag="table0", align_bytes=64)
-        nc.sync.dma_start(out=v_table[:], in_=words(v_words[0]))
 
         column_ps = psum.tile([P, P], F32, name="column_ps", tag="bank5")
         nc.tensor.transpose(column_ps[:], gate_rows[:], ident[:])
@@ -185,6 +183,9 @@ def tile_picked_zcbow_relu_p_kernel(
                 gate_sb[d][:, part * count : (part + 1) * count],
                 ALU.mult,
             )
+
+        v_table = reused.tile([P, G], I32, name="v_table", offset=8192, align_bytes=64)
+        nc.sync.dma_start(out=v_table[:], in_=words(v_words[0]))
 
         h_sb = {}
         for tile_no in range(ROW_TILES):

@@ -43,10 +43,10 @@ def tile_picked_zcbow_relu_p_kernel(
         offs_sb = keep.tile([P, S // LIST], U16, name="offs_sb")
         pos_sb = [keep.tile([P, V // LIST], U16, name="pos_sb%d" % d) for d in range(2)]
         cand_sb = keep.tile([P, R // LIST], U16, name="cand_sb")
-        x_table = [keep.tile([P, T], I32, name="x_table%d" % g, tag="table%d" % g, align_bytes=64) for g in range(PASSES)]
-        xs_table = keep.tile([P, T], U8, name="xs_table", align_bytes=64)
-        vs_table = keep.tile([P, G], U8, name="vs_table")
-        x_scale = keep.tile([P, PASSES, S], U8, name="x_scale", align_bytes=64)
+        x_table = [keep.tile([P, T], I32, name="x_table%d" % g, tag="table%d" % g, align_bytes=256) for g in range(PASSES)]
+        xs_table = keep.tile([P, T], U8, name="xs_table", align_bytes=256)
+        vs_table = keep.tile([P, G], U8, name="vs_table", align_bytes=256)
+        x_scale = keep.tile([P, PASSES, S], U8, name="x_scale", align_bytes=256)
         ident = keep.tile([P, P], F32, name="ident")
         gate_rows = keep.tile([P, P], F32, name="gate_rows")
 
@@ -89,9 +89,9 @@ def tile_picked_zcbow_relu_p_kernel(
                 w_codes[g, first_tile + n] = codes[:, n * P : (n + 1) * P]
                 w_scale[g, first_tile + n] = scale[:, n * P : (n + 1) * P]
 
-        w_first = keep.tile([P, PACK, H], F32, name="w_first")
-        w_low = reused.tile([P, PACK, HALF], F32, name="w_low", offset=8192, align_bytes=64)
-        w_high = keep.tile([P, PACK, HALF], F32, name="w_high", tag="w_high", align_bytes=64)
+        w_first = keep.tile([P, PACK, H], F32, name="w_first", align_bytes=256)
+        w_low = reused.tile([P, PACK, HALF], F32, name="w_low", offset=8192, align_bytes=256)
+        w_high = keep.tile([P, PACK, HALF], F32, name="w_high", tag="w_high", align_bytes=256)
         nc.sync.dma_start(out=x_table[0][:, 0:HEAD], in_=words(x_words[0])[:, 0:HEAD])
         nc.sync.dma_start(offs_sb[:], offs)
         nc.sync.dma_start(out=xs_table[0 : P : SPREAD // 2].bitcast(I32), in_=x_scales.rearrange("g n c -> n g c").bitcast(I32))
@@ -102,7 +102,7 @@ def tile_picked_zcbow_relu_p_kernel(
         nc.sync.dma_start(out=gate_rows[0:4, :], in_=gate[:, 0, :].rearrange("d (w c) -> d w c", c=P))
         nc.sync.dma_start(out=x_table[1][:], in_=words(x_words[1]))
 
-        xs_picked = keep.tile([P, S], U8, name="xs_picked")
+        xs_picked = keep.tile([P, S], U8, name="xs_picked", align_bytes=256)
         nc.vector.tensor_copy(xs_picked[:], xs_table[:].indirect(offs_sb[:]))
         for q in range(4):
             nc.sync.dma_start(
@@ -114,7 +114,7 @@ def tile_picked_zcbow_relu_p_kernel(
         nc.sync.dma_start(pos_sb[0][:], pos1)
         nc.sync.dma_start(pos_sb[1][:], pos2)
 
-        vs_picked = keep.tile([P, R], U8, name="vs_picked")
+        vs_picked = keep.tile([P, R], U8, name="vs_picked", align_bytes=256)
         nc.vector.tensor_copy(vs_picked[:], vs_table[:].indirect(cand_sb[:]))
 
         x_codes = []
@@ -184,7 +184,7 @@ def tile_picked_zcbow_relu_p_kernel(
                 ALU.mult,
             )
 
-        v_table = reused.tile([P, G], I32, name="v_table", offset=8192, align_bytes=64)
+        v_table = reused.tile([P, G], I32, name="v_table", offset=8192, align_bytes=256)
         nc.sync.dma_start(out=v_table[:], in_=words(v_words[0]))
 
         h_sb = {}
@@ -230,7 +230,7 @@ def tile_picked_zcbow_relu_p_kernel(
                 in_=vs_picked[SPREAD * r + SPREAD // 2 : P : QUADRANT].bitcast(I32),
             )
 
-        terms = keep.tile([P, 2, ROW_TILES + 2, P], F32, name="terms", tag="w_high", align_bytes=64)
+        terms = keep.tile([P, 2, ROW_TILES + 2, P], F32, name="terms", tag="w_high", align_bytes=256)
         for d in range(2):
             gather_term(terms[:, d, 2, :], h_sb[1], d, 0, WINDOW_TILES)
         for d in range(2):
@@ -338,6 +338,6 @@ def tile_picked_zcbow_relu_p_kernel(
             nc.scalar.activation(out=exps[:], in_=y_ps[w][:], func=ACT.Exp, bias=neg_max[:], accum_out=total[:])
             inv_total = keep.tile([P, 1], F32, name="inv_total%d" % w)
             nc.vector.reciprocal(out=inv_total[:], in_=total[:])
-            probs = keep.tile([P, R], F32, name="probs%d" % w)
+            probs = keep.tile([P, R], F32, name="probs%d" % w, align_bytes=256)
             nc.vector.tensor_scalar(out=probs[:], in0=exps[:], scalar1=inv_total[:], scalar2=None, op0=ALU.mult)
             nc.sync.dma_start(out=out[w * P : (w + 1) * P, :], in_=probs[:])

@@ -23,11 +23,10 @@ SPREAD = 8
 PASSES = K // (P * PACK)
 WINDOW_TILES = V // P
 ROW_TILES = H // P
-PARTS = 2
 HALF = H // 2
-HEAD = T // 2
+QUARTER = H // 4
 QUADS = HALF // 4
-SCALAR_QUADS = 24
+SCALAR_QUADS = 28
 FLOPS = 2 * K * H * S + 2 * H * V * R
 
 
@@ -89,16 +88,21 @@ def tile_picked_zcbow_relu_p_kernel(
                 w_codes[g, first_tile + n] = codes[:, n * P : (n + 1) * P]
                 w_scale[g, first_tile + n] = scale[:, n * P : (n + 1) * P]
 
-        w_first = keep.tile([P, PACK, H], F32, name="w_first", align_bytes=256)
-        w_low = reused.tile([P, PACK, HALF], F32, name="w_low", offset=8192, align_bytes=256)
-        w_high = keep.tile([P, PACK, HALF], F32, name="w_high", tag="w_high", align_bytes=256)
-        nc.sync.dma_start(out=x_table[0][:, 0:HEAD], in_=words(x_words[0])[:, 0:HEAD])
+        def raw_tile(name, columns):
+            return keep.tile([P, PACK, columns], F32, name=name, align_bytes=256)
+
+        w_low = [raw_tile("w_low%d" % g, HALF) for g in range(PASSES)]
+        w_third = [
+            raw_tile("w_third0", QUARTER),
+            reused.tile([P, PACK, QUARTER], F32, name="w_third1", offset=10240, align_bytes=256),
+        ]
+        w_fourth = [raw_tile("w_fourth%d" % g, QUARTER) for g in range(PASSES)]
+        nc.sync.dma_start(out=w_low[0][:], in_=w_rows(0)[:, :, 0:HALF])
         nc.sync.dma_start(offs_sb[:], offs)
         nc.sync.dma_start(out=xs_table[0 : P : SPREAD // 2].bitcast(I32), in_=x_scales.rearrange("g n c -> n g c").bitcast(I32))
         nc.sync.dma_start(cand_sb[:], cand)
         nc.sync.dma_start(out=vs_table[SPREAD // 2 : P : SPREAD].bitcast(I32), in_=v_scales[0].bitcast(I32))
-        nc.sync.dma_start(out=w_first[:], in_=w_rows(0))
-        nc.sync.dma_start(out=x_table[0][:, HEAD:T], in_=words(x_words[0])[:, HEAD:T])
+        nc.sync.dma_start(out=x_table[0][:], in_=words(x_words[0]))
         nc.sync.dma_start(out=gate_rows[0:4, :], in_=gate[:, 0, :].rearrange("d (w c) -> d w c", c=P))
         nc.sync.dma_start(out=x_table[1][:], in_=words(x_words[1]))
 
@@ -109,11 +113,18 @@ def tile_picked_zcbow_relu_p_kernel(
                 out=x_scale[QUADRANT * q : QUADRANT * q + 4].bitcast(I32),
                 in_=xs_picked[QUADRANT * q : QUADRANT * (q + 1) : SPREAD // 2].bitcast(I32),
             )
-        nc.sync.dma_start(out=w_low[:], in_=w_rows(1)[:, :, 0:HALF])
-        nc.sync.dma_start(out=w_high[:], in_=w_rows(1)[:, :, HALF:H])
+        nc.sync.dma_start(out=w_low[1][:], in_=w_rows(1)[:, :, 0:HALF])
+        for g in range(PASSES):
+            nc.sync.dma_start(out=w_third[g][:], in_=w_rows(g)[:, :, HALF : HALF + QUARTER])
+        for g in range(PASSES):
+            nc.sync.dma_start(out=w_fourth[g][:], in_=w_rows(g)[:, :, HALF + QUARTER : H])
         nc.sync.dma_start(pos_sb[0][:], pos1)
         nc.sync.dma_start(pos_sb[1][:], pos2)
+        v_table = reused.tile([P, G], I32, name="v_table", offset=10240, align_bytes=256)
 
+        grouped = grouped_tile("grouped_low0", 2, "grouped_low0")
+        group_w(nc.scalar.copy, grouped[:], w_low[0][:], slice(0, QUADS))
+        quantise_w(grouped[:], 0, 0)
         vs_picked = keep.tile([P, R], U8, name="vs_picked", align_bytes=256)
         nc.vector.tensor_copy(vs_picked[:], vs_table[:].indirect(cand_sb[:]))
 
@@ -127,33 +138,26 @@ def tile_picked_zcbow_relu_p_kernel(
                     x_codes[g][:, entries], x_table[g][:].bitcast(U32).indirect(list_part(offs_sb, part, parts))
                 )
 
-        grouped = [grouped_tile("grouped_first%d" % half, 2, "grouped_first%d" % half) for half in range(2)]
-        for half in range(2):
-            group_w(nc.scalar.copy, grouped[half][:], w_first[:, :, half * HALF : (half + 1) * HALF], slice(0, QUADS))
-        quantise_w(grouped[0][:], 0, 0)
         gather_x(0, 1)
-        quantise_w(grouped[1][:], 0, 2)
 
         column_ps = psum.tile([P, P], F32, name="column_ps", tag="bank5")
         nc.tensor.transpose(column_ps[:], gate_rows[:], ident[:])
         gate_column = keep.tile([P, 4], F32, name="gate_column")
         nc.scalar.copy(out=gate_column[:], in_=column_ps[:, 0:4])
-        first_gate = reused.tile([P, 1], F32, name="first_gate", offset=1536, align_bytes=64)
-        nc.scalar.copy(out=first_gate[:], in_=column_ps[:, 1:2])
         gate_ps = psum.tile([P, 4, P], F32, name="gate_ps", tag="bank6")
         for c in range(4):
             nc.tensor.transpose(gate_ps[:, c, :], gate_column[:, c : c + 1].to_broadcast([P, P]), ident[:])
         gate_sb = [
-            reused.tile([P, V], F32, name="gate_sb0", offset=6656, align_bytes=64),
+            reused.tile([P, V], F32, name="gate_sb0", offset=6656, align_bytes=256),
             keep.tile([P, V], F32, name="gate_sb1"),
         ]
         for d in range(2):
             nc.scalar.copy(out=gate_sb[d][:], in_=gate_ps[:, 2 * d : 2 * d + 2, :].rearrange("p c t -> p (c t)"))
 
         gather_x(1, 1)
-        grouped = grouped_tile("grouped_low", 2, "grouped_low")
-        group_w(nc.scalar.copy, grouped[:], w_low[:], slice(0, SCALAR_QUADS))
-        group_w(nc.vector.tensor_copy, grouped[:], w_low[:], slice(SCALAR_QUADS, QUADS))
+        grouped = grouped_tile("grouped_low1", 2, "grouped_low1")
+        group_w(nc.scalar.copy, grouped[:], w_low[1][:], slice(0, SCALAR_QUADS))
+        group_w(nc.vector.tensor_copy, grouped[:], w_low[1][:], slice(SCALAR_QUADS, QUADS))
         for u in (1, 0):
             quantise_w(grouped[:, u * P * PACK : (u + 1) * P * PACK], 1, u)
 
@@ -175,6 +179,31 @@ def tile_picked_zcbow_relu_p_kernel(
                 sums.append(h_ps)
             return sums
 
+        h_sb = {}
+        for tile_no in range(ROW_TILES):
+            h_sb[tile_no] = keep.tile([P, S], F32, name="h_sb%d" % tile_no, align_bytes=64)
+
+        def row_tile(tile_no, banks):
+            parts = len(banks)
+            for part, sums in enumerate(first_product(tile_no, parts, banks)):
+                entries = slice(part * S // parts, (part + 1) * S // parts)
+                nc.scalar.activation(out=h_sb[tile_no][:, entries], in_=sums[:], func=ACT.Relu)
+
+        grouped_third = [grouped_tile("grouped_third%d" % g, 1, "grouped_third%d" % g) for g in range(PASSES)]
+        whole_quarter = slice(0, QUARTER // 4)
+        group_w(nc.scalar.copy, grouped_third[0][:], w_third[0][:], whole_quarter)
+        group_w(nc.vector.tensor_copy, grouped_third[1][:], w_third[1][:], whole_quarter)
+        nc.sync.dma_start(out=v_table[:], in_=words(v_words[0]))
+        for g in range(PASSES):
+            quantise_w(grouped_third[g][:], g, 2)
+        row_tile(1, ["bank0", "bank1"])
+        row_tile(0, ["bank2"])
+        row_tile(2, ["bank3"])
+
+        grouped_fourth = grouped_tile("grouped_fourth", PASSES, "grouped_fourth")
+        for g in range(PASSES):
+            group_w(nc.vector.tensor_copy, grouped_fourth[:, g * P * PACK : (g + 1) * P * PACK], w_fourth[g][:], whole_quarter)
+
         def gather_term(term, h_tile, d, part, parts):
             count = V // parts
             nc.vector.tensor_tensor(
@@ -184,44 +213,21 @@ def tile_picked_zcbow_relu_p_kernel(
                 ALU.mult,
             )
 
-        v_table = reused.tile([P, G], I32, name="v_table", offset=8192, align_bytes=256)
-        nc.sync.dma_start(out=v_table[:], in_=words(v_words[0]))
+        terms = keep.tile([P, 2, ROW_TILES + 2, P], F32, name="terms", align_bytes=64)
+        gather_term(terms[:, 0, 1, :], h_sb[1], 0, 0, WINDOW_TILES)
+        quantise_w(grouped_fourth[:], PASSES, 0)
+        for g in range(PASSES):
+            w_codes[g, 3], w_scale[g, 3] = w_codes[PASSES, g], w_scale[PASSES, g]
+        row_tile(3, ["bank4", "bank7"])
 
-        h_sb = {}
-        for tile_no in range(ROW_TILES):
-            h_sb[tile_no] = keep.tile([P, S], F32, name="h_sb%d" % tile_no, align_bytes=64)
-
-        def relu_whole(tile_no, bank):
-            nc.scalar.activation(out=h_sb[tile_no][:], in_=first_product(tile_no, 1, [bank])[0][:], func=ACT.Relu)
-
-        halves = first_product(1, PARTS, ["bank0", "bank1"])
-        grouped = grouped_tile("grouped_high", 2, "grouped_high")
-        group_w(nc.vector.tensor_copy, grouped[:], w_high[:], slice(0, QUADS))
-        nc.scalar.activation(out=h_sb[1][:, 0 : S // 2], in_=halves[0][:], func=ACT.Relu)
-        nc.vector.tensor_scalar(out=h_sb[1][:, S // 2 : S], in0=halves[1][:], scalar1=0.0, scalar2=None, op0=ALU.max)
-        quantise_w(grouped[:], 1, 2)
-        relu_whole(0, "bank2")
-
-        plain = [
-            reused.tile([P, 2, P], F32, name="plain%d" % d, offset=(3072, 512)[d], align_bytes=64) for d in range(2)
-        ]
-
-        def slot(tile_no):
-            return 2 * (tile_no % 2) + tile_no // 2
-
-        def gather_plain(tile_no, d):
-            nc.scalar.activation(
-                out=plain[d][:, slot(tile_no) - 1, :],
-                in_=h_sb[tile_no][:].indirect(list_part(pos_sb[d], 1, WINDOW_TILES)),
-                func=ACT.Copy,
-            )
-
+        plain = keep.tile([P, 2, 2, P], F32, name="plain", align_bytes=64)
         for d in range(2):
-            gather_plain(1, d)
-        relu_whole(2, "bank3")
-        relu_whole(3, "bank4")
-        for d in range(2):
-            gather_plain(2, d)
+            for tile_no in (1, 0):
+                nc.scalar.activation(
+                    out=plain[:, d, tile_no, :],
+                    in_=h_sb[tile_no][:].indirect(list_part(pos_sb[d], 1, WINDOW_TILES)),
+                    func=ACT.Copy,
+                )
 
         v_scale = x_scale[4:P, 0, :]
         for r in range(4):
@@ -230,79 +236,69 @@ def tile_picked_zcbow_relu_p_kernel(
                 in_=vs_picked[SPREAD * r + SPREAD // 2 : P : QUADRANT].bitcast(I32),
             )
 
-        terms = keep.tile([P, 2, ROW_TILES + 2, P], F32, name="terms", tag="w_high", align_bytes=256)
+        gather_term(terms[:, 1, 1, :], h_sb[1], 1, 0, WINDOW_TILES)
         for d in range(2):
-            gather_term(terms[:, d, 2, :], h_sb[1], d, 0, WINDOW_TILES)
+            gather_term(terms[:, d, 0, :], h_sb[0], d, 0, WINDOW_TILES)
         for d in range(2):
-            gather_term(terms[:, d, 0:2, :].rearrange("p w c -> p (w c)"), h_sb[0], d, 0, 1)
-        for tile_no in (2, 3):
+            gather_term(terms[:, d, 2:4, :].rearrange("p w c -> p (w c)"), h_sb[2], d, 0, 1)
+        for w in range(WINDOW_TILES):
             for d in range(2):
-                gather_term(terms[:, d, tile_no + 1, :], h_sb[tile_no], d, 0, WINDOW_TILES)
-        for d in range(2):
-            gather_term(terms[:, d, 5, :], h_sb[3], d, 1, WINDOW_TILES)
+                gather_term(terms[:, d, 4 + w, :], h_sb[3], d, w, WINDOW_TILES)
 
-        plain_ps = [psum.tile([P, 2, P], F32, name="plain_ps%d" % d, tag="bank%d" % (3 + d)) for d in range(2)]
-        sums_ps = psum.tile([P, 3, P], F32, name="sums_ps", tag="bank5")
+        early = P + QUARTER // 2
+        sums_ps = psum.tile([P, 2, early], F32, name="sums_ps", tag="bank4")
+        plain_ps = psum.tile([P, 2, 2, P], F32, name="plain_ps", tag="bank7")
         other_ps = psum.tile([P, P], F32, name="other_ps", tag="bank6")
         last_ps = [psum.tile([P, P], F32, name="last_ps%d" % w, tag="bank%d" % w) for w in range(WINDOW_TILES)]
 
-        def turn_term(target, place, d):
-            nc.tensor.matmul(
-                target, lhsT=terms[:, d, place, :], rhs=ident[:], is_transpose=True, start=(d == 0), stop=(d == 1)
-            )
+        def turn_terms(target, place):
+            for d in range(2):
+                nc.tensor.matmul(
+                    target, lhsT=terms[:, d, place, :], rhs=ident[:], is_transpose=True, start=(d == 0), stop=(d == 1)
+                )
 
-        def turn_plain(tile_no, d):
-            place = slot(tile_no) - 1
-            nc.tensor.transpose(plain_ps[d][:, place, :], plain[d][:, place, :], ident[:])
-
+        for u in (1, 0):
+            turn_terms(sums_ps[:, u, 0:P], u)
         for d in range(2):
-            turn_term(sums_ps[:, slot(1), :], 2, d)
-        for d in range(2):
-            turn_term(sums_ps[:, slot(0), :], 0, d)
-            turn_term(other_ps[:], 1, d)
-        for d in range(2):
-            turn_plain(1, d)
-            turn_term(sums_ps[:, slot(2), :], 3, d)
-        for d in range(2):
-            turn_term(last_ps[0][:], 4, d)
-            turn_plain(2, d)
-        for d in range(2):
-            turn_term(last_ps[1][:], 5, d)
+            for u in (1, 0):
+                nc.tensor.transpose(plain_ps[:, d, u, :], plain[:, d, u, :], ident[:])
+        turn_terms(sums_ps[:, :, P:early], 2)
+        turn_terms(other_ps[:], 3)
+        for w in range(WINDOW_TILES):
+            turn_terms(last_ps[w][:], 4 + w)
 
         z_rows = [
-            keep.tile([P, ROW_TILES, P], BF16, name="z_rows0"),
-            reused.tile([P, ROW_TILES, P], BF16, name="z_rows1", offset=3072, align_bytes=64),
+            keep.tile([P, 2, 2 * P], BF16, name="z_rows0"),
+            reused.tile([P, 2, 2 * P], BF16, name="z_rows1", offset=6144, align_bytes=256),
         ]
-        v_codes = [
-            reused.tile([P, R // 2], U32, name="v_codes%d" % part, offset=(7168, 1024)[part], align_bytes=64)
-            for part in range(2)
-        ]
+        v_codes = reused.tile([P, R], U32, name="v_codes", offset=7168, align_bytes=256)
 
-        def gather_v(part):
-            nc.vector.tensor_copy(v_codes[part][:], v_table[:].bitcast(U32).indirect(list_part(cand_sb, part, 2)))
-
-        nc.scalar.copy(out=z_rows[0][:, 0:3, :], in_=sums_ps[:])
-        gather_v(0)
         first_term = keep.tile([P, 2, P], F32, name="first_term")
-        nc.scalar.activation(out=first_term[:], in_=plain_ps[0][:], func=ACT.Copy, scale=first_gate[:])
+        nc.scalar.activation(out=first_term[:], in_=plain_ps[:, 0], func=ACT.Copy, scale=gate_column[:, 1:2])
+        nc.scalar.copy(out=z_rows[0][:, :, 0:early], in_=sums_ps[:])
         nc.vector.scalar_tensor_tensor(
-            out=z_rows[1][:, 1:3, :],
-            in0=plain_ps[1][:],
+            out=z_rows[1][:, :, 0:P],
+            in0=plain_ps[:, 1],
             scalar=gate_column[:, 3:4],
             in1=first_term[:],
             op0=ALU.mult,
             op1=ALU.add,
         )
-        gather_v(1)
-        nc.scalar.copy(out=z_rows[0][:, 3, :], in_=last_ps[0][:])
-        nc.scalar.copy(out=z_rows[1][:, 0, :], in_=other_ps[:])
-        nc.scalar.copy(out=z_rows[1][:, 3, :], in_=last_ps[1][:])
+        for part in range(2):
+            picked = slice(part * R // 2, (part + 1) * R // 2)
+            nc.vector.tensor_copy(v_codes[:, picked], v_table[:].bitcast(U32).indirect(list_part(cand_sb, part, 2)))
 
-        back_ps = [psum.tile([P, 2, P], F32, name="back_ps%d" % w, tag="bank%d" % (2 - 2 * w)) for w in range(WINDOW_TILES)]
+        def round_quarter(w, start, sums):
+            nc.scalar.copy(out=z_rows[w][:, :, start : start + QUARTER // 2], in_=sums[:].rearrange("t (u c) -> t u c", u=2))
+
+        round_quarter(0, early, last_ps[0])
+        round_quarter(1, P, other_ps)
+        round_quarter(1, early, last_ps[1])
+
+        back_ps = [psum.tile([P, 2, P], F32, name="back_ps%d" % w, tag="bank%d" % (2 + w)) for w in range(WINDOW_TILES)]
         for w in range(WINDOW_TILES):
             for u in range(2):
-                pairs = z_rows[w][:, 2 * u : 2 * u + 2, :].rearrange("t r c -> t (r c)").bitcast(F32)
-                nc.tensor.transpose(back_ps[w][:, u, :], pairs, ident[:])
+                nc.tensor.transpose(back_ps[w][:, u, :], z_rows[w][:, u, :].bitcast(F32), ident[:])
 
         z_grouped = []
         for w in range(WINDOW_TILES):
@@ -317,14 +313,14 @@ def tile_picked_zcbow_relu_p_kernel(
             z_codes = keep.tile([P, P], U32, name="z_codes%d" % w, align_bytes=64)
             z_scale = keep.tile([P, P], U8, name="z_scale%d" % w, align_bytes=64)
             nc.vector.quantize_mx(out=z_codes[:].bitcast(FP8X4), scales=z_scale[:], in_=z_grouped[w][:])
-            y_ps.append(psum.tile([P, R], F32, name="y_ps%d" % w, tag="bank%d" % (7 - 2 * w)))
+            y_ps.append(psum.tile([P, R], F32, name="y_ps%d" % w, tag="bank%d" % (5 - w)))
             for part in range(2):
                 picked = slice(part * R // 2, (part + 1) * R // 2)
                 nc.tensor.matmul_mx(
                     out=y_ps[w][:, picked],
                     lhsT=z_codes[:].bitcast(FP8X4),
                     lhsT_scale=z_scale[:],
-                    rhs=v_codes[part][:].bitcast(FP8X4),
+                    rhs=v_codes[:, picked].bitcast(FP8X4),
                     rhs_scale=v_scale[:, picked],
                     start=True,
                     stop=True,

@@ -100,9 +100,9 @@ def tile_picked_zcbow_relu_p_kernel(
         nc.sync.dma_start(out=w_low[0][:], in_=w_rows(0)[:, :, 0:HALF])
         nc.sync.dma_start(offs_sb[:], offs)
         nc.sync.dma_start(out=xs_table[0 : P : SPREAD // 2].bitcast(I32), in_=x_scales.rearrange("g n c -> n g c").bitcast(I32))
+        nc.sync.dma_start(out=x_table[0][:], in_=words(x_words[0]))
         nc.sync.dma_start(cand_sb[:], cand)
         nc.sync.dma_start(out=vs_table[SPREAD // 2 : P : SPREAD].bitcast(I32), in_=v_scales[0].bitcast(I32))
-        nc.sync.dma_start(out=x_table[0][:], in_=words(x_words[0]))
         nc.sync.dma_start(out=gate_rows[0:4, :], in_=gate[:, 0, :].rearrange("d (w c) -> d w c", c=P))
         nc.sync.dma_start(out=x_table[1][:], in_=words(x_words[1]))
 
@@ -125,8 +125,6 @@ def tile_picked_zcbow_relu_p_kernel(
         grouped = grouped_tile("grouped_low0", 2, "grouped_low0")
         group_w(nc.scalar.copy, grouped[:], w_low[0][:], slice(0, QUADS))
         quantise_w(grouped[:], 0, 0)
-        vs_picked = keep.tile([P, R], U8, name="vs_picked", align_bytes=256)
-        nc.vector.tensor_copy(vs_picked[:], vs_table[:].indirect(cand_sb[:]))
 
         x_codes = []
 
@@ -139,6 +137,8 @@ def tile_picked_zcbow_relu_p_kernel(
                 )
 
         gather_x(0, 1)
+        vs_picked = keep.tile([P, R], U8, name="vs_picked", align_bytes=256)
+        nc.vector.tensor_copy(vs_picked[:], vs_table[:].indirect(cand_sb[:]))
 
         column_ps = psum.tile([P, P], F32, name="column_ps", tag="bank5")
         nc.tensor.transpose(column_ps[:], gate_rows[:], ident[:])
@@ -220,11 +220,14 @@ def tile_picked_zcbow_relu_p_kernel(
             w_codes[g, 3], w_scale[g, 3] = w_codes[PASSES, g], w_scale[PASSES, g]
         row_tile(3, ["bank4", "bank7"])
 
-        plain = keep.tile([P, 2, 2, P], F32, name="plain", align_bytes=64)
+        plain = [
+            keep.tile([P, 2, P], F32, name="plain0", align_bytes=64),
+            keep.tile([P, 2, P], F32, name="plain1", tag="w_codes%d0" % PASSES, align_bytes=64),
+        ]
         for d in range(2):
             for tile_no in (1, 0):
                 nc.scalar.activation(
-                    out=plain[:, d, tile_no, :],
+                    out=plain[d][:, tile_no, :],
                     in_=h_sb[tile_no][:].indirect(list_part(pos_sb[d], 1, WINDOW_TILES)),
                     func=ACT.Copy,
                 )
@@ -247,7 +250,7 @@ def tile_picked_zcbow_relu_p_kernel(
 
         early = P + QUARTER // 2
         sums_ps = psum.tile([P, 2, early], F32, name="sums_ps", tag="bank4")
-        plain_ps = psum.tile([P, 2, 2, P], F32, name="plain_ps", tag="bank7")
+        plain_ps = [psum.tile([P, 2, P], F32, name="plain_ps%d" % d, tag="bank%d" % (7, 3)[d]) for d in range(2)]
         other_ps = psum.tile([P, P], F32, name="other_ps", tag="bank6")
         last_ps = [psum.tile([P, P], F32, name="last_ps%d" % w, tag="bank%d" % w) for w in range(WINDOW_TILES)]
 
@@ -261,7 +264,7 @@ def tile_picked_zcbow_relu_p_kernel(
             turn_terms(sums_ps[:, u, 0:P], u)
         for d in range(2):
             for u in (1, 0):
-                nc.tensor.transpose(plain_ps[:, d, u, :], plain[:, d, u, :], ident[:])
+                nc.tensor.transpose(plain_ps[d][:, u, :], plain[d][:, u, :], ident[:])
         turn_terms(sums_ps[:, :, P:early], 2)
         turn_terms(other_ps[:], 3)
         for w in range(WINDOW_TILES):
@@ -274,11 +277,11 @@ def tile_picked_zcbow_relu_p_kernel(
         v_codes = reused.tile([P, R], U32, name="v_codes", offset=7168, align_bytes=256)
 
         first_term = keep.tile([P, 2, P], F32, name="first_term")
-        nc.scalar.activation(out=first_term[:], in_=plain_ps[:, 0], func=ACT.Copy, scale=gate_column[:, 1:2])
+        nc.scalar.activation(out=first_term[:], in_=plain_ps[0][:], func=ACT.Copy, scale=gate_column[:, 1:2])
         nc.scalar.copy(out=z_rows[0][:, :, 0:early], in_=sums_ps[:])
         nc.vector.scalar_tensor_tensor(
             out=z_rows[1][:, :, 0:P],
-            in0=plain_ps[:, 1],
+            in0=plain_ps[1][:],
             scalar=gate_column[:, 3:4],
             in1=first_term[:],
             op0=ALU.mult,

@@ -200,6 +200,17 @@ def tile_picked_zcbow_relu_p_kernel(
         row_tile(0, ["bank2"])
         row_tile(2, ["bank3"])
 
+        warm_ps = psum.tile([P, S], F32, name="warm_ps", tag="bank5")
+        nc.tensor.matmul_mx(
+            out=warm_ps[:],
+            lhsT=w_codes[0, 0].bitcast(FP8X4),
+            lhsT_scale=w_scale[0, 0],
+            rhs=x_codes[0][:].bitcast(FP8X4),
+            rhs_scale=x_scale[:, 0, :],
+            start=True,
+            stop=True,
+        )
+
         grouped_fourth = grouped_tile("grouped_fourth", PASSES, "grouped_fourth")
         for g in range(PASSES):
             group_w(nc.vector.tensor_copy, grouped_fourth[:, g * P * PACK : (g + 1) * P * PACK], w_fourth[g][:], whole_quarter)

@@ -349,5 +349,7 @@ def tile_picked_zcbow_relu_p_kernel(
             inv_total = keep.tile([P, 1], F32, name="inv_total%d" % w)
             nc.vector.reciprocal(out=inv_total[:], in_=total[:])
             probs = keep.tile([P, R], F32, name="probs%d" % w, align_bytes=256)
-            nc.vector.tensor_scalar(out=probs[:], in0=exps[:], scalar1=inv_total[:], scalar2=None, op0=ALU.mult)
-            nc.sync.dma_start(out=out[w * P : (w + 1) * P, :], in_=probs[:])
+            for part in range(2):
+                picked = slice(part * R // 2, (part + 1) * R // 2)
+                nc.vector.tensor_scalar(out=probs[:, picked], in0=exps[:, picked], scalar1=inv_total[:], scalar2=None, op0=ALU.mult)
+                nc.sync.dma_start(out=out[w * P : (w + 1) * P, picked], in_=probs[:, picked])

@@ -260,8 +260,8 @@ def tile_picked_zcbow_relu_p_kernel(
                 gather_term(terms[:, d, 4 + w, :], h_sb[3], d, w, WINDOW_TILES)
 
         early = P + QUARTER // 2
-        sums_ps = psum.tile([P, 2, early], F32, name="sums_ps", tag="bank4")
-        plain_ps = [psum.tile([P, 2, P], F32, name="plain_ps%d" % d, tag="bank%d" % (7, 3)[d]) for d in range(2)]
+        sums_ps = psum.tile([P, 2, early], F32, name="sums_ps", tag="bank5")
+        plain_ps = [psum.tile([P, 2, P], F32, name="plain_ps%d" % d, tag="bank%d" % (4, 3)[d]) for d in range(2)]
         other_ps = psum.tile([P, P], F32, name="other_ps", tag="bank6")
         last_ps = [psum.tile([P, P], F32, name="last_ps%d" % w, tag="bank%d" % w) for w in range(WINDOW_TILES)]
 
@@ -327,7 +327,7 @@ def tile_picked_zcbow_relu_p_kernel(
             z_codes = keep.tile([P, P], U32, name="z_codes%d" % w, align_bytes=64)
             z_scale = keep.tile([P, P], U8, name="z_scale%d" % w, align_bytes=64)
             nc.vector.quantize_mx(out=z_codes[:].bitcast(FP8X4), scales=z_scale[:], in_=z_grouped[w][:])
-            y_ps.append(psum.tile([P, R], F32, name="y_ps%d" % w, tag="bank%d" % (5 - w)))
+            y_ps.append(psum.tile([P, R], F32, name="y_ps%d" % w, tag="bank%d" % (7 - 2 * w)))
             for part in range(2):
                 picked = slice(part * R // 2, (part + 1) * R // 2)
                 nc.tensor.matmul_mx(

from contextlib import ExitStack

import concourse.mybir as mybir
from concourse.masks import make_identity

F32 = mybir.dt.float32
BF16 = mybir.dt.bfloat16
I32 = mybir.dt.int32
U32 = mybir.dt.uint32
U16 = mybir.dt.uint16
U8 = mybir.dt.uint8
FP8X4 = mybir.dt.float8_e4m3fn_x4
ALU = mybir.AluOpType
ACT = mybir.ActivationFunctionType
AXIS = mybir.AxisListType

K, T, S, V, H, G, R = 1024, 2048, 512, 256, 512, 2048, 512
P = 128
PACK = 4
LIST = 16
QUADRANT = 32
SPREAD = 8
PASSES = K // (P * PACK)
WINDOW_TILES = V // P
ROW_TILES = H // P
HALF = H // 2
QUARTER = H // 4
QUADS = HALF // 4
SCALAR_QUADS = 28
FLOPS = 2 * K * H * S + 2 * H * V * R


def tile_picked_zcbow_relu_p_kernel(
    tc, x_words, x_scales, w1, gate, v_words, v_scales, offs, pos1, pos2, cand, out
):
    nc = tc.nc
    with ExitStack() as ctx:
        keep = ctx.enter_context(tc.tile_pool(name="keep", bufs=1))
        reused = ctx.enter_context(tc.tile_pool(name="reused", bufs=1))
        psum = ctx.enter_context(tc.psum_pool(name="psum", bufs=1))

        offs_sb = keep.tile([P, S // LIST], U16, name="offs_sb")
        pos_sb = [keep.tile([P, V // LIST], U16, name="pos_sb%d" % d) for d in range(2)]
        cand_sb = keep.tile([P, R // LIST], U16, name="cand_sb")
        x_table = [keep.tile([P, T], I32, name="x_table%d" % g, tag="table%d" % g, align_bytes=256) for g in range(PASSES)]
        xs_table = keep.tile([P, T], U8, name="xs_table", align_bytes=256)
        vs_table = keep.tile([P, G], U8, name="vs_table", align_bytes=256)
        x_scale = keep.tile([P, PASSES, S], U8, name="x_scale", align_bytes=256)
        ident = keep.tile([P, P], F32, name="ident")
        gate_rows = keep.tile([P, P], F32, name="gate_rows")

        nc.vector.memset(xs_table[:].bitcast(I32), 0)
        nc.vector.memset(vs_table[:].bitcast(I32), 0)
        nc.vector.memset(ident[:], 0.0)
        nc.vector.memset(gate_rows[:], 0.0)
        nc.vector.memset(x_scale[:].bitcast(I32), 0)
        make_identity(nc, ident[:], nomemset=True)

        def words(table):
            return table.rearrange("p n j -> p (n j)").bitcast(I32)

        def list_part(list_sb, part, parts):
            columns = list_sb.shape[1] // parts
            return list_sb[:, part * columns : (part + 1) * columns]

        def w_rows(g):
            return w1[g * P * PACK : (g + 1) * P * PACK, :].rearrange("(p j) c -> p j c", j=PACK)

        def group_w(engine_copy, grouped, columns, quads):
            engine_copy(
                out=grouped.rearrange("p (u m e j) -> p m j u e", u=2, e=2, j=PACK)[:, quads],
                in_=columns.rearrange("p j (m u e) -> p m j u e", u=2, e=2)[:, quads],
            )

        def grouped_tile(name, row_tiles, tag):
            return keep.tile([P, row_tiles * P * PACK], BF16, name=name, tag=tag, align_bytes=64)

        w_codes = {}
        w_scale = {}

        def quantise_w(grouped, g, first_tile):
            count = grouped.shape[1] // PACK
            name = "%d%d" % (g, first_tile)
            codes = keep.tile([P, count], U32, name="w_codes" + name, tag="w_codes" + name, align_bytes=64)
            scale = keep.tile([P, count], U8, name="w_scale" + name, align_bytes=64)
            nc.vector.quantize_mx(out=codes[:].bitcast(FP8X4), scales=scale[:], in_=grouped)
            for n in range(count // P):
                w_codes[g, first_tile + n] = codes[:, n * P : (n + 1) * P]
                w_scale[g, first_tile + n] = scale[:, n * P : (n + 1) * P]

        def raw_tile(name, columns):
            return keep.tile([P, PACK, columns], F32, name=name, align_bytes=256)

        w_low = [raw_tile("w_low%d" % g, HALF) for g in range(PASSES)]
        w_third = [
            raw_tile("w_third0", QUARTER),
            reused.tile([P, PACK, QUARTER], F32, name="w_third1", offset=10240, align_bytes=256),
        ]
        w_fourth = [raw_tile("w_fourth%d" % g, QUARTER) for g in range(PASSES)]
        nc.sync.dma_start(out=w_low[0][:], in_=w_rows(0)[:, :, 0:HALF])
        nc.sync.dma_start(offs_sb[:], offs)
        nc.sync.dma_start(out=xs_table[0 : P : SPREAD // 2].bitcast(I32), in_=x_scales.rearrange("g n c -> n g c").bitcast(I32))
        nc.sync.dma_start(out=x_table[0][:], in_=words(x_words[0]))
        nc.sync.dma_start(cand_sb[:], cand)
        nc.sync.dma_start(out=vs_table[SPREAD // 2 : P : SPREAD].bitcast(I32), in_=v_scales[0].bitcast(I32))
        nc.sync.dma_start(out=gate_rows[0:4, :], in_=gate[:, 0, :].rearrange("d (w c) -> d w c", c=P))
        nc.sync.dma_start(out=x_table[1][:], in_=words(x_words[1]))

        xs_picked = keep.tile([P, S], U8, name="xs_picked", align_bytes=256)
        nc.vector.tensor_copy(xs_picked[:], xs_table[:].indirect(offs_sb[:]))
        for q in range(4):
            nc.sync.dma_start(
                out=x_scale[QUADRANT * q : QUADRANT * q + 4].bitcast(I32),
                in_=xs_picked[QUADRANT * q : QUADRANT * (q + 1) : SPREAD // 2].bitcast(I32),
            )
        nc.sync.dma_start(out=w_low[1][:], in_=w_rows(1)[:, :, 0:HALF])
        for g in range(PASSES):
            nc.sync.dma_start(out=w_third[g][:], in_=w_rows(g)[:, :, HALF : HALF + QUARTER])
        for g in range(PASSES):
            nc.sync.dma_start(out=w_fourth[g][:], in_=w_rows(g)[:, :, HALF + QUARTER : H])
        nc.sync.dma_start(pos_sb[0][:], pos1)
        nc.sync.dma_start(pos_sb[1][:], pos2)
        v_table = reused.tile([P, G], I32, name="v_table", offset=10240, align_bytes=256)

        grouped = grouped_tile("grouped_low0", 2, "grouped_low0")
        group_w(nc.scalar.copy, grouped[:], w_low[0][:], slice(0, QUADS))
        quantise_w(grouped[:], 0, 0)

        x_codes = []

        def gather_x(g, parts):
            x_codes.append(keep.tile([P, S], U32, name="x_codes%d" % g, align_bytes=64))
            for part in range(parts):
                entries = slice(part * S // parts, (part + 1) * S // parts)
                nc.vector.tensor_copy(
                    x_codes[g][:, entries], x_table[g][:].bitcast(U32).indirect(list_part(offs_sb, part, parts))
                )

        gather_x(0, 1)
        vs_picked = keep.tile([P, R], U8, name="vs_picked", align_bytes=256)
        nc.vector.tensor_copy(vs_picked[:], vs_table[:].indirect(cand_sb[:]))

        column_ps = psum.tile([P, P], F32, name="column_ps", tag="bank5")
        nc.tensor.transpose(column_ps[:], gate_rows[:], ident[:])
        gate_column = keep.tile([P, 4], F32, name="gate_column")
        nc.scalar.copy(out=gate_column[:], in_=column_ps[:, 0:4])
        gate_ps = psum.tile([P, 4, P], F32, name="gate_ps", tag="bank6")
        for c in range(4):
            nc.tensor.transpose(gate_ps[:, c, :], gate_column[:, c : c + 1].to_broadcast([P, P]), ident[:])
        gate_sb = [
            reused.tile([P, V], F32, name="gate_sb0", offset=6656, align_bytes=256),
            keep.tile([P, V], F32, name="gate_sb1"),
        ]
        for d in range(2):
            nc.scalar.copy(out=gate_sb[d][:], in_=gate_ps[:, 2 * d : 2 * d + 2, :].rearrange("p c t -> p (c t)"))

        gather_x(1, 1)
        grouped = grouped_tile("grouped_low1", 2, "grouped_low1")
        group_w(nc.scalar.copy, grouped[:], w_low[1][:], slice(0, SCALAR_QUADS))
        group_w(nc.vector.tensor_copy, grouped[:], w_low[1][:], slice(SCALAR_QUADS, QUADS))
        for u in (1, 0):
            quantise_w(grouped[:, u * P * PACK : (u + 1) * P * PACK], 1, u)

        def first_product(tile_no, parts, banks):
            sums = []
            for part in range(parts):
                entries = slice(part * S // parts, (part + 1) * S // parts)
                h_ps = psum.tile([P, S // parts], F32, name="h_ps%d%d" % (tile_no, part), tag=banks[part])
                for g in range(PASSES):
                    nc.tensor.matmul_mx(
                        out=h_ps[:],
                        lhsT=w_codes[g, tile_no].bitcast(FP8X4),
                        lhsT_scale=w_scale[g, tile_no],
                        rhs=x_codes[g][:, entries].bitcast(FP8X4),
                        rhs_scale=x_scale[:, g, entries],
                        start=(g == 0),
                        stop=(g == PASSES - 1),
                    )
                sums.append(h_ps)
            return sums

        h_sb = {}
        for tile_no in range(ROW_TILES):
            h_sb[tile_no] = keep.tile([P, S], F32, name="h_sb%d" % tile_no, align_bytes=64)

        def row_tile(tile_no, banks):
            parts = len(banks)
            for part, sums in enumerate(first_product(tile_no, parts, banks)):
                entries = slice(part * S // parts, (part + 1) * S // parts)
                nc.scalar.activation(out=h_sb[tile_no][:, entries], in_=sums[:], func=ACT.Relu)

        grouped_third = [grouped_tile("grouped_third%d" % g, 1, "grouped_third%d" % g) for g in range(PASSES)]
        whole_quarter = slice(0, QUARTER // 4)
        group_w(nc.scalar.copy, grouped_third[0][:], w_third[0][:], whole_quarter)
        group_w(nc.vector.tensor_copy, grouped_third[1][:], w_third[1][:], whole_quarter)
        nc.sync.dma_start(out=v_table[:], in_=words(v_words[0]))
        for g in range(PASSES):
            quantise_w(grouped_third[g][:], g, 2)
        row_tile(1, ["bank0", "bank1"])
        row_tile(0, ["bank2"])
        row_tile(2, ["bank3"])

        warm_ps = psum.tile([P, S], F32, name="warm_ps", tag="bank5")
        nc.tensor.matmul_mx(
            out=warm_ps[:],
            lhsT=w_codes[0, 0].bitcast(FP8X4),
            lhsT_scale=w_scale[0, 0],
            rhs=x_codes[0][:].bitcast(FP8X4),
            rhs_scale=x_scale[:, 0, :],
            start=True,
            stop=True,
        )

        grouped_fourth = grouped_tile("grouped_fourth", PASSES, "grouped_fourth")
        for g in range(PASSES):
            group_w(nc.vector.tensor_copy, grouped_fourth[:, g * P * PACK : (g + 1) * P * PACK], w_fourth[g][:], whole_quarter)

        def gather_term(term, h_tile, d, part, parts):
            count = V // parts
            nc.vector.tensor_tensor(
                term,
                h_tile[:].indirect(list_part(pos_sb[d], part, parts)),
                gate_sb[d][:, part * count : (part + 1) * count],
                ALU.mult,
            )

        terms = keep.tile([P, 2, ROW_TILES + 2, P], F32, name="terms", align_bytes=64)
        gather_term(terms[:, 0, 1, :], h_sb[1], 0, 0, WINDOW_TILES)
        quantise_w(grouped_fourth[:], PASSES, 0)
        for g in range(PASSES):
            w_codes[g, 3], w_scale[g, 3] = w_codes[PASSES, g], w_scale[PASSES, g]
        row_tile(3, ["bank4", "bank7"])

        plain = [
            keep.tile([P, 2, P], F32, name="plain0", align_bytes=64),
            keep.tile([P, 2, P], F32, name="plain1", tag="w_codes%d0" % PASSES, align_bytes=64),
        ]
        for d in range(2):
            for tile_no in (1, 0):
                nc.scalar.activation(
                    out=plain[d][:, tile_no, :],
                    in_=h_sb[tile_no][:].indirect(list_part(pos_sb[d], 1, WINDOW_TILES)),
                    func=ACT.Copy,
                )

        v_scale = x_scale[4:P, 0, :]
        for r in range(4):
            nc.sync.dma_start(
                out=x_scale[4 + r : P : QUADRANT, 0, :].bitcast(I32),
                in_=vs_picked[SPREAD * r + SPREAD // 2 : P : QUADRANT].bitcast(I32),
            )

        gather_term(terms[:, 1, 1, :], h_sb[1], 1, 0, WINDOW_TILES)
        for d in range(2):
            gather_term(terms[:, d, 0, :], h_sb[0], d, 0, WINDOW_TILES)
        for d in range(2):
            gather_term(terms[:, d, 2:4, :].rearrange("p w c -> p (w c)"), h_sb[2], d, 0, 1)
        for w in range(WINDOW_TILES):
            for d in range(2):
                gather_term(terms[:, d, 4 + w, :], h_sb[3], d, w, WINDOW_TILES)

        early = P + QUARTER // 2
        sums_ps = psum.tile([P, 2, early], F32, name="sums_ps", tag="bank5")
        plain_ps = [psum.tile([P, 2, P], F32, name="plain_ps%d" % d, tag="bank%d" % (4, 3)[d]) for d in range(2)]
        other_ps = psum.tile([P, P], F32, name="other_ps", tag="bank6")
        last_ps = [psum.tile([P, P], F32, name="last_ps%d" % w, tag="bank%d" % w) for w in range(WINDOW_TILES)]

        def turn_terms(target, place):
            for d in range(2):
                nc.tensor.matmul(
                    target, lhsT=terms[:, d, place, :], rhs=ident[:], is_transpose=True, start=(d == 0), stop=(d == 1)
                )

        for u in (1, 0):
            turn_terms(sums_ps[:, u, 0:P], u)
        for d in range(2):
            for u in (1, 0):
                nc.tensor.transpose(plain_ps[d][:, u, :], plain[d][:, u, :], ident[:])
        turn_terms(sums_ps[:, :, P:early], 2)
        turn_terms(other_ps[:], 3)
        for w in range(WINDOW_TILES):
            turn_terms(last_ps[w][:], 4 + w)

        z_rows = [
            keep.tile([P, 2, 2 * P], BF16, name="z_rows0"),
            reused.tile([P, 2, 2 * P], BF16, name="z_rows1", offset=6144, align_bytes=256),
        ]
        v_codes = reused.tile([P, R], U32, name="v_codes", offset=7168, align_bytes=256)

        first_term = keep.tile([P, 2, P], F32, name="first_term")
        nc.scalar.activation(out=first_term[:], in_=plain_ps[0][:], func=ACT.Copy, scale=gate_column[:, 1:2])
        nc.scalar.copy(out=z_rows[0][:, :, 0:early], in_=sums_ps[:])
        nc.vector.scalar_tensor_tensor(
            out=z_rows[1][:, :, 0:P],
            in0=plain_ps[1][:],
            scalar=gate_column[:, 3:4],
            in1=first_term[:],
            op0=ALU.mult,
            op1=ALU.add,
        )
        for part in range(2):
            picked = slice(part * R // 2, (part + 1) * R // 2)
            nc.vector.tensor_copy(v_codes[:, picked], v_table[:].bitcast(U32).indirect(list_part(cand_sb, part, 2)))

        def round_quarter(w, start, sums):
            nc.scalar.copy(out=z_rows[w][:, :, start : start + QUARTER // 2], in_=sums[:].rearrange("t (u c) -> t u c", u=2))

        round_quarter(0, early, last_ps[0])
        round_quarter(1, P, other_ps)
        round_quarter(1, early, last_ps[1])

        back_ps = [psum.tile([P, 2, P], F32, name="back_ps%d" % w, tag="bank%d" % (2 + w)) for w in range(WINDOW_TILES)]
        for w in range(WINDOW_TILES):
            for u in range(2):
                nc.tensor.transpose(back_ps[w][:, u, :], z_rows[w][:, u, :].bitcast(F32), ident[:])

        z_grouped = []
        for w in range(WINDOW_TILES):
            z_grouped.append(keep.tile([P, P * PACK], BF16, name="z_grouped%d" % w, align_bytes=64))
            nc.scalar.copy(
                out=z_grouped[w][:].bitcast(F32).rearrange("p (t u) -> p t u", u=2),
                in_=back_ps[w][:].rearrange("p u t -> p t u"),
            )

        y_ps = []
        for w in range(WINDOW_TILES):
            z_codes = keep.tile([P, P], U32, name="z_codes%d" % w, align_bytes=64)
            z_scale = keep.tile([P, P], U8, name="z_scale%d" % w, align_bytes=64)
            nc.vector.quantize_mx(out=z_codes[:].bitcast(FP8X4), scales=z_scale[:], in_=z_grouped[w][:])
            y_ps.append(psum.tile([P, R], F32, name="y_ps%d" % w, tag="bank%d" % (7 - 2 * w)))
            for part in range(2):
                picked = slice(part * R // 2, (part + 1) * R // 2)
                nc.tensor.matmul_mx(
                    out=y_ps[w][:, picked],
                    lhsT=z_codes[:].bitcast(FP8X4),
                    lhsT_scale=z_scale[:],
                    rhs=v_codes[:, picked].bitcast(FP8X4),
                    rhs_scale=v_scale[:, picked],
                    start=True,
                    stop=True,
                )

        for w in range(WINDOW_TILES):
            neg_max = keep.tile([P, 1], F32, name="neg_max%d" % w)
            nc.vector.tensor_reduce(out=neg_max[:], in_=y_ps[w][:], axis=AXIS.X, op=ALU.max, negate=True)
            exps = keep.tile([P, R], F32, name="exps%d" % w)
            total = keep.tile([P, 1], F32, name="total%d" % w)
            nc.scalar.activation(out=exps[:], in_=y_ps[w][:], func=ACT.Exp, bias=neg_max[:], accum_out=total[:])
            inv_total = keep.tile([P, 1], F32, name="inv_total%d" % w)
            nc.vector.reciprocal(out=inv_total[:], in_=total[:])
            probs = keep.tile([P, R], F32, name="probs%d" % w, align_bytes=256)
            for part in range(2):
                picked = slice(part * R // 2, (part + 1) * R // 2)
                nc.vector.tensor_scalar(out=probs[:, picked], in0=exps[:, picked], scalar1=inv_total[:], scalar2=None, op0=ALU.mult)
                nc.sync.dma_start(out=out[w * P : (w + 1) * P, picked], in_=probs[:, picked])
